import numpy as np
import ml_dtypes


def mxq(x, axis, fmt="e4m3"):
    dtype, down = {"e4m3": (ml_dtypes.float8_e4m3fn, 7), "e5m2": (ml_dtypes.float8_e5m2, 14)}[fmt]
    v = np.moveaxis(np.asarray(x, np.float32).astype(ml_dtypes.bfloat16).astype(np.float64), axis, -1)
    blocks = v.reshape(v.shape[:-1] + (-1, 32))
    amax = np.abs(blocks).max(-1, keepdims=True)
    byte = np.maximum(np.where(amax > 0, np.frexp(amax)[1] - 1 + 127, 0) - down, 1)
    scale = np.exp2(byte - 127.0)
    codes = (blocks / scale).astype(np.float32).astype(dtype).astype(np.float64)
    return np.moveaxis((codes * scale).reshape(v.shape), -1, axis)


WIDE = False


def mx_kscale(k):
    if not WIDE:
        return np.ones(k)
    levels = np.array([10, -10, 5, -5, 0])
    if k % 512:
        return np.exp2(np.random.permutation(np.resize(levels, k // 32))).repeat(32)
    a = np.empty((k // 512, 16))
    for p in range(k // 512):
        a[p, :8] = np.random.permutation(np.resize(levels, 8))
        for g in range(8):
            far = levels[np.abs(levels - a[p, g]) >= 10]
            a[p, g + 8] = far[np.random.randint(len(far))]
    return np.exp2(a.ravel()).repeat(32)


def f64(x):
    return np.asarray(x).astype(np.float64)


def striped(idx):
    return np.tile(idx.reshape(-1, 16).T, (8, 1)).astype(np.uint16)


def unstriped(offs):
    return offs[:16].T.reshape(-1).astype(np.int64)


E2M1 = np.array([0.0, 0.5, 1.0, 1.5, 2.0, 3.0, 4.0, 6.0, -0.0, -0.5, -1.0, -1.5, -2.0, -3.0, -4.0, -6.0])


def pack_weight(w, fmt):
    k, n = w.shape
    w = f64(np.asarray(w, np.float32).astype(ml_dtypes.bfloat16)).reshape(k // 32, 32, n)
    amax = np.abs(w).max(1)
    if fmt == "e4m3":
        byte = np.frexp(amax)[1] - 1 + 127 - 7
    else:
        mant, ex = np.frexp(amax / 6.0)
        byte = np.where(mant > 0.5, ex, ex - 1) + 127
    byte = np.clip(np.where(amax > 0, byte, 1), 1, 254)
    scaled = (w * np.exp2(127.0 - byte)[:, None, :]).reshape(k, n).astype(np.float32)
    by_word = np.ascontiguousarray(scaled.reshape(k // 512, 128, 4, n).transpose(0, 1, 3, 2))
    if fmt == "e4m3":
        words = by_word.astype(ml_dtypes.float8_e4m3fn).view(np.uint8)
    else:
        c = by_word.astype(ml_dtypes.float4_e2m1fn).view(np.uint8) & 0xF
        words = (c[..., 0::2] | (c[..., 1::2] << 4)).reshape(k // 512, 128, 2 * n)
    return np.ascontiguousarray(words), np.ascontiguousarray(byte.astype(np.uint8).reshape(k // 512, 16, n))


def unpack_weight(words, scales, fmt):
    g, _, n = scales.shape
    words = np.ascontiguousarray(words).reshape(g, 128, n, -1)
    if fmt == "e4m3":
        vals = words.view(ml_dtypes.float8_e4m3fn).astype(np.float64)
    else:
        nib = np.empty((g, 128, n, 4), np.uint8)
        nib[..., 0::2] = words & 0xF
        nib[..., 1::2] = words >> 4
        vals = E2M1[nib]
    vals = vals * np.repeat(np.exp2(scales.astype(np.float64) - 127.0), 8, axis=1)[..., None]
    return vals.transpose(0, 1, 3, 2).reshape(g * 512, n)


def gelu(v):
    return 0.5 * v * (1.0 + np.tanh(np.sqrt(2.0 / np.pi) * (v + 0.044715 * v**3)))


def striped8(idx):
    return np.concatenate([v.reshape(-1, 16).T for v in idx]).astype(np.uint16)


def unstriped8(offs):
    return np.stack([offs[16 * g:16 * g + 16].T.reshape(-1) for g in range(8)]).astype(np.int64)


def runs(v, idx8):
    k = np.arange(v.shape[0])
    return v[k[:, None], idx8[k % 512 // 64]]


def put_heads(h, wgs, idx8, t2):
    r = np.arange(h.shape[0])
    page = np.zeros((h.shape[0], t2))
    page[r[:, None], idx8[r % 512 // 64]] = wgs[r // 4 % 128] * h
    return page


K, H, N, T, S, T2 = 512, 1024, 512, 2048, 1024, 2048

def setup_inputs():
    n = np.random.standard_normal
    s = mx_kscale(K)[:, None]
    u = mx_kscale(H)[:, None]
    base = n((K, H))
    wa = (base + n((K, H))) / np.sqrt(2 * K) / s * u.T
    wb = (base + n((K, H))) / np.sqrt(2 * K) / s * u.T
    wc = (base + n((K, H))) / np.sqrt(2 * K) / s * u.T
    tab_words, tab_scales = pack_weight(n((K, T)) * s, "e4m3")
    wb_words, wb_scales = pack_weight(wb, "e2m1")
    wc_words, wc_scales = pack_weight(wc, "e4m3")
    return {
        "tab_words": tab_words, "tab_scales": tab_scales,
        "offs": striped8(np.stack([np.random.permutation(T)[:S] for _ in range(8)])),
        "wa": wa.astype(np.float32),
        "wb_words": wb_words, "wb_scales": wb_scales,
        "wc_words": wc_words, "wc_scales": wc_scales,
        "wd": (1.2 * n((H, N)) / np.sqrt(H) / u).astype(np.float32),
        "gd": np.random.uniform(0.5, 2.0, N).astype(np.float32),
        "bd": (0.5 * n(N)).astype(np.float32),
        "wgo": np.repeat(np.random.uniform(0.5, 2.0, (8, S)), 16, axis=0).astype(np.float32),
        "offs2": striped8(np.stack([np.random.permutation(T2)[:S] for _ in range(8)])),
    }

def reference(tab_words, tab_scales, offs, wa, wb_words, wb_scales, wc_words, wc_scales, wd, gd, bd, wgo, offs2):
    v = runs(unpack_weight(tab_words, tab_scales, "e4m3"), unstriped8(offs))
    a = mxq(f64(wa), 0, "e4m3").T @ v
    b = unpack_weight(wb_words, wb_scales, "e2m1").T @ v
    c = unpack_weight(wc_words, wc_scales, "e4m3").T @ v
    h = np.maximum(np.minimum(a, b), np.minimum(np.maximum(a, b), c))
    y = mxq(f64(wd), 0, "e4m3").T @ mxq(h, 0, "e4m3")
    y = y * f64(gd)[:, None] + f64(bd)[:, None]
    return put_heads(y, f64(wgo), unstriped8(offs2), T2)

@@ -1,0 +1,235 @@
+from contextlib import ExitStack
+
+import concourse.mybir as mybir
+
+K, H, N, T, S, T2 = 512, 1024, 512, 2048, 1024, 2048
+FLOPS = 2 * S * (3 * K * H + H * N)
+
+F32 = mybir.dt.float32
+BF16 = mybir.dt.bfloat16
+I32 = mybir.dt.int32
+U32 = mybir.dt.uint32
+U16 = mybir.dt.uint16
+U8 = mybir.dt.uint8
+FP8X4 = mybir.dt.float8_e4m3fn_x4
+FP4X4 = mybir.dt.float4_e2m1fn_x4
+ALU = mybir.AluOpType
+IDENT = mybir.ActivationFunctionType.Identity
+
+P = 128
+PASS = 512
+HB = H // PASS
+CH = 256
+NCH = S // CH
+UN = 128
+
+
+def tile_list_median_codeword_repair_kernel(
+    tc, tab_words, tab_scales, offs, wa, wb_words, wb_scales, wc_words, wc_scales, wd, gd, bd, wgo, offs2, out
+):
+    nc = tc.nc
+    with ExitStack() as ctx:
+        keep = ctx.enter_context(tc.tile_pool(name="keep", bufs=1))
+        ring = ctx.enter_context(tc.tile_pool(name="ring", bufs=3))
+        psum = ctx.enter_context(tc.psum_pool(name="psum", bufs=2))
+
+        def kept(shape, dtype, name):
+            return keep.tile(shape, dtype, name=name, align_bytes=64)
+
+        idx = kept([P, S // 16], U16, "idx")
+        idx2 = kept([P, S // 16], U16, "idx2")
+        nc.sync.dma_start(idx[:], offs)
+
+        tab_sc = kept([P, T], U8, "tab_sc")
+        w_sc = kept([P, 2 * H], U8, "w_sc")
+        nc.vector.memset(tab_sc[:].bitcast(I32), 0)
+        nc.gpsimd.memset(w_sc[:].bitcast(I32), 0)
+
+        def staged(shape, dtype, name, tag):
+            return keep.tile(shape, dtype, name=name, tag=tag, align_bytes=64)
+
+        wa_raw = [staged([P, 4, PASS], F32, "wa_raw0", "stage_a")]
+        wc_raw = [staged([P, PASS], I32, "wc_raw0", "stage_c"), kept([P, PASS], I32, "wc_raw1")]
+        wb_raw = [staged([P, PASS // 2], I32, "wb_raw0", "stage_b"), kept([P, PASS // 2], I32, "wb_raw1")]
+        tab = staged([P, T], U32, "tab", "stage_p3")
+        wa_v = wa.rearrange("(p j) c -> p j c", j=4)
+        wc_v = wc_words[0].rearrange("p n t -> p (n t)").bitcast(I32)
+        wb_v = wb_words[0].bitcast(I32)
+
+        def load_w(b):
+            nc.sync.dma_start(wc_raw[b][:], wc_v[:, b * PASS : (b + 1) * PASS])
+            nc.sync.dma_start(wb_raw[b][:], wb_v[:, b * PASS // 2 : (b + 1) * PASS // 2])
+
+        gain = kept([P, 4], F32, "gain")
+        bias = kept([P, 4], F32, "bias")
+        for j in range(2):
+            nc.sync.dma_start(wa_raw[0][:, 2 * j : 2 * j + 2, :], wa_v[:, 2 * j : 2 * j + 2, 0:PASS])
+        nc.sync.dma_start(idx2[:], offs2)
+        nc.sync.dma_start(gain[:], gd.rearrange("(p i) -> p i", i=4))
+        nc.sync.dma_start(bias[:], bd.rearrange("(p i) -> p i", i=4))
+        nc.scalar.dma_start(tab_sc[0:P:8, :].bitcast(I32), tab_scales[0].bitcast(I32))
+        nc.scalar.dma_start(w_sc[0:P:8, 0:H].bitcast(I32), wb_scales[0].bitcast(I32))
+        nc.scalar.dma_start(w_sc[0:P:8, H : 2 * H].bitcast(I32), wc_scales[0].bitcast(I32))
+        nc.sync.dma_start(tab[:].bitcast(I32), tab_words[0].rearrange("p n t -> p (n t)").bitcast(I32))
+        load_w(0)
+
+        g_sc = kept([P, S], U8, "g_sc")
+        nc.vector.tensor_copy(g_sc[:], tab_sc[:].indirect(idx[:]))
+        planes = kept([P, S + 2 * H], U8, "planes")
+        nc.vector.tensor_copy(
+            planes[:, S:].bitcast(I32).rearrange("p (a t c) -> p a t c", t=4, c=32),
+            w_sc[:].bitcast(I32).rearrange("p (a c t) -> p a t c", t=4, c=32),
+        )
+        nc.vector.tensor_copy(planes[:, 0:S].bitcast(I32), g_sc[:].bitcast(I32))
+        for r in range(1, 4):
+            nc.scalar.dma_start(planes[r:P:32, :].bitcast(I32), planes[8 * r : P : 32, :].bitcast(I32))
+
+        load_w(1)
+        wd_raw = []
+
+        def load_wd(b, tag):
+            wd_raw.append(staged([P, 4, N], F32, f"wd_raw{b}", tag))
+            rows = wd[b * PASS : (b + 1) * PASS, :].rearrange("(c t v) n -> v c t n", t=4, v=4)
+            for v in range(4):
+                nc.sync.dma_start(wd_raw[b][v:P:4, :, :], rows[v])
+
+
+        wa16 = [staged([P, 4 * PASS], BF16, "wa16_0", "stage_p2"), kept([P, 4 * PASS], BF16, "wa16_1")]
+        wa_q = [kept([P, PASS], U32, f"wa_q{b}") for b in range(HB)]
+        wa_s = [kept([P, PASS], U8, f"wa_s{b}") for b in range(HB)]
+        wc_q = [kept([P, PASS], I32, f"wc_q{b}") for b in range(HB)]
+        wb_q = [kept([P, PASS // 2], I32, f"wb_q{b}") for b in range(HB)]
+
+        def prep_w(b):
+            src = wa_raw[b][:].rearrange("p j (c t v) -> p t c v j", t=4, v=4)
+            dst = wa16[b][:].rearrange("p (t c v j) -> p t c v j", t=4, v=4, j=4)
+            nc.scalar.activation(dst[:, 0], src[:, 0], IDENT)
+            nc.scalar.copy(dst[:, 1:4], src[:, 1:4])
+            nc.vector.tensor_copy(
+                wc_q[b][:].rearrange("p (t c v) -> p t c v", t=4, v=4),
+                wc_raw[b][:].rearrange("p (c t v) -> p t c v", t=4, v=4),
+            )
+            nc.vector.tensor_copy(
+                wb_q[b][:].rearrange("p (t c v) -> p t c v", t=4, v=2),
+                wb_raw[b][:].rearrange("p (c t v) -> p t c v", t=4, v=2),
+            )
+            nc.vector.quantize_mx(wa_q[b][:].bitcast(FP8X4), wa_s[b][:], wa16[b][:])
+
+        g_w = kept([P, S], U32, "g_w")
+
+        def gather_words(c):
+            nc.vector.tensor_copy(g_w[:, c * CH : (c + 1) * CH], tab[:].indirect(idx[:, c * CH // 16 : (c + 1) * CH // 16]))
+
+        wd16 = [kept([P, 4 * N], BF16, f"wd16_{b}") for b in range(HB)]
+        wd_q = [kept([P, N], U32, f"wd_q{b}") for b in range(HB)]
+        wd_s = [kept([P, N], U8, f"wd_s{b}") for b in range(HB)]
+
+        def prep_wd(b):
+            src = wd_raw[b][:].rearrange("p t (m i) -> p m i t", i=4)
+            dst = wd16[b][:].rearrange("p (i m t) -> p m i t", i=4, t=4)
+            nc.scalar.copy(dst, src)
+            nc.vector.quantize_mx(wd_q[b][:].bitcast(FP8X4), wd_s[b][:], wd16[b][:])
+
+        pages = [kept([P, T2], F32, f"page{i}") for i in range(2)]
+        pages += [staged([P, T2], F32, f"page{i}", f"stage_p{i}") for i in (2, 3)]
+        y = [kept([P, S], F32, f"y{i}") for i in range(4)]
+        h_q = [kept([P, HB, CH], U32, f"h_q{c}") for c in range(NCH)]
+        h_s = [kept([P, HB, CH], U8, f"h_s{c}") for c in range(NCH)]
+
+        def estimates(c, b):
+            est = [ring.tile([P, 4 * CH], BF16, name=f"est{w}", align_bytes=64) for w in range(3)]
+            for u in range(CH // UN):
+                j0 = c * CH + u * UN
+                rhs = g_w[:, j0 : j0 + UN].bitcast(FP8X4)
+                rhs_s = planes[:, j0 : j0 + UN]
+                for w in range(3):
+                    bank = psum.tile([P, 4, UN], F32, name=f"bank{w}")
+                    for t in range(4):
+                        cols = slice(t * P, (t + 1) * P)
+                        if w == 0:
+                            lhs = wb_q[b][:, t * P // 2 : (t + 1) * P // 2].bitcast(FP4X4)
+                            lhs_s = planes[:, S + b * PASS + t * P : S + b * PASS + (t + 1) * P]
+                        elif w == 1:
+                            lhs = wc_q[b][:, cols].bitcast(FP8X4)
+                            lhs_s = planes[:, S + H + b * PASS + t * P : S + H + b * PASS + (t + 1) * P]
+                        else:
+                            lhs = wa_q[b][:, cols].bitcast(FP8X4)
+                            lhs_s = wa_s[b][:, cols]
+                        nc.tensor.matmul_mx(bank[:, t, :], lhsT=lhs, lhsT_scale=lhs_s, rhs=rhs, rhs_scale=rhs_s, start=True, stop=True)
+                    nc.scalar.copy(
+                        est[w][:, 4 * u * UN : 4 * (u + 1) * UN].rearrange("p (n t) -> p n t", t=4),
+                        bank[:].rearrange("p t n -> p n t"),
+                    )
+            return est
+
+        def vote(c, b, est):
+            lo = ring.tile([P, 4 * CH], BF16, name="lo", align_bytes=64)
+            hi = ring.tile([P, 4 * CH], BF16, name="hi", align_bytes=64)
+            mid = ring.tile([P, 4 * CH], BF16, name="mid", align_bytes=64)
+            h16 = ring.tile([P, 4 * CH], BF16, name="h16", align_bytes=64)
+            nc.vector.tensor_tensor(hi[:], est[0][:], est[1][:], ALU.max)
+            nc.vector.tensor_tensor(lo[:], est[0][:], est[1][:], ALU.min)
+            nc.vector.tensor_tensor(mid[:], hi[:], est[2][:], ALU.min)
+            nc.vector.tensor_tensor(h16[:], lo[:], mid[:], ALU.max)
+            nc.vector.quantize_mx(h_q[c][:, b, :].bitcast(FP8X4), h_s[c][:, b, :], h16[:])
+
+        def back(c):
+            for half in range(2):
+                bank = psum.tile([P, 2, CH], F32, name="bank_y")
+                for e in range(2):
+                    i = 2 * half + e
+                    cols = slice(i * P, (i + 1) * P)
+                    for b in range(HB):
+                        nc.tensor.matmul_mx(
+                            bank[:, e, :],
+                            lhsT=wd_q[b][:, cols].bitcast(FP8X4),
+                            lhsT_scale=wd_s[b][:, cols],
+                            rhs=h_q[c][:, b, :].bitcast(FP8X4),
+                            rhs_scale=h_s[c][:, b, :],
+                            start=(b == 0),
+                            stop=(b == HB - 1),
+                        )
+                for e in range(2):
+                    i = 2 * half + e
+                    nc.scalar.activation(
+                        y[i][:, c * CH : (c + 1) * CH], bank[:, e, :], IDENT, bias=bias[:, i : i + 1], scale=gain[:, i : i + 1]
+                    )
+
+        def place(i, j0, j1):
+            nc.vector.tensor_tensor(
+                pages[i][:].indirect(idx2[:, j0 // 16 : j1 // 16]), y[i][:, j0:j1], wgo_sb[:, j0:j1], ALU.mult
+            )
+
+        out_v = out.rearrange("(p i) t -> p i t", i=4)
+
+        prep_w(0)
+        wa_raw.append(staged([P, 4, PASS], F32, "wa_raw1", "stage_a"))
+        nc.sync.dma_start(wa_raw[1][:], wa_v[:, :, PASS : 2 * PASS])
+        load_wd(0, "stage_c")
+        wgo_sb = staged([P, S], F32, "wgo_sb", "stage_b")
+        gather_words(0)
+        est = estimates(0, 0)
+        prep_w(1)
+        load_wd(1, "stage_a")
+        nc.sync.dma_start(wgo_sb[:], wgo)
+        vote(0, 0, est)
+        for c in range(1, NCH):
+            gather_words(c)
+        est = estimates(0, 1)
+        vote(0, 1, est)
+        for b in range(HB):
+            prep_wd(b)
+        for i in range(4):
+            nc.vector.memset(pages[i][:].bitcast(I32), 0)
+        for c in range(1, NCH + 1):
+            if c < NCH:
+                for b in range(HB):
+                    est = estimates(c, b)
+                    vote(c, b, est)
+            back(c - 1)
+            for i in range(3):
+                place(i, (c - 1) * CH, c * CH)
+        for i in range(3):
+            nc.sync.dma_start(out_v[:, i, :], pages[i][:])
+        place(3, 0, S)
+        nc.sync.dma_start(out_v[:, 3, :], pages[3][:])

@@ -36,44 +36,49 @@ def tile_list_median_codeword_repair_kernel(
         def kept(shape, dtype, name):
             return keep.tile(shape, dtype, name=name, align_bytes=64)
 
+        def staged(shape, dtype, name, tag):
+            return keep.tile(shape, dtype, name=name, tag=tag, align_bytes=64)
+
         idx = kept([P, S // 16], U16, "idx")
         idx2 = kept([P, S // 16], U16, "idx2")
         nc.sync.dma_start(idx[:], offs)
 
-        tab_sc = kept([P, T], U8, "tab_sc")
-        w_sc = kept([P, 2 * H], U8, "w_sc")
+        tab_sc = staged([P, T], U8, "tab_sc", "stage_s")
+        w_sc = staged([P, 2 * H], U8, "w_sc", "stage_w")
         nc.vector.memset(tab_sc[:].bitcast(I32), 0)
         nc.gpsimd.memset(w_sc[:].bitcast(I32), 0)
-
-        def staged(shape, dtype, name, tag):
-            return keep.tile(shape, dtype, name=name, tag=tag, align_bytes=64)
-
-        wa_raw = [staged([P, 4, PASS], F32, "wa_raw0", "stage_a")]
-        wc_raw = [staged([P, PASS], I32, "wc_raw0", "stage_c"), kept([P, PASS], I32, "wc_raw1")]
-        wb_raw = [staged([P, PASS // 2], I32, "wb_raw0", "stage_b"), kept([P, PASS // 2], I32, "wb_raw1")]
-        tab = staged([P, T], U32, "tab", "stage_p3")
-        wa_v = wa.rearrange("(p j) c -> p j c", j=4)
-        wc_v = wc_words[0].rearrange("p n t -> p (n t)").bitcast(I32)
-        wb_v = wb_words[0].bitcast(I32)
-
-        def load_w(b):
-            nc.sync.dma_start(wc_raw[b][:], wc_v[:, b * PASS : (b + 1) * PASS])
-            nc.sync.dma_start(wb_raw[b][:], wb_v[:, b * PASS // 2 : (b + 1) * PASS // 2])
-
-        gain = kept([P, 4], F32, "gain")
-        bias = kept([P, 4], F32, "bias")
-        for j in range(2):
-            nc.sync.dma_start(wa_raw[0][:, 2 * j : 2 * j + 2, :], wa_v[:, 2 * j : 2 * j + 2, 0:PASS])
-        nc.sync.dma_start(idx2[:], offs2)
-        nc.sync.dma_start(gain[:], gd.rearrange("(p i) -> p i", i=4))
-        nc.sync.dma_start(bias[:], bd.rearrange("(p i) -> p i", i=4))
         nc.scalar.dma_start(tab_sc[0:P:8, :].bitcast(I32), tab_scales[0].bitcast(I32))
         nc.scalar.dma_start(w_sc[0:P:8, 0:H].bitcast(I32), wb_scales[0].bitcast(I32))
         nc.scalar.dma_start(w_sc[0:P:8, H : 2 * H].bitcast(I32), wc_scales[0].bitcast(I32))
-        nc.sync.dma_start(tab[:].bitcast(I32), tab_words[0].rearrange("p n t -> p (n t)").bitcast(I32))
-        load_w(0)
 
-        g_sc = kept([P, S], U8, "g_sc")
+        tab = kept([P, T], U32, "tab")
+        wa_v = wa.rearrange("(p j) c -> p j c", j=4)
+        wc_v = wc_words[0].rearrange("p n t -> p (n t)").bitcast(I32)
+        wb_v = wb_words[0].bitcast(I32)
+        wa_raw, wb_raw, wc_raw, wd_raw = [], [], [], []
+
+        def load_packed(b):
+            wb_raw.append(staged([P, PASS // 2], I32, f"wb_raw{b}", f"stage_b{b}"))
+            wc_raw.append(staged([P, PASS], I32, f"wc_raw{b}", "stage_c"))
+            nc.sync.dma_start(wb_raw[b][:], wb_v[:, b * PASS // 2 : (b + 1) * PASS // 2])
+            nc.sync.dma_start(wc_raw[b][:], wc_v[:, b * PASS : (b + 1) * PASS])
+
+        def load_wa(b, tag):
+            wa_raw.append(staged([P, 4, PASS], F32, f"wa_raw{b}", tag))
+            nc.sync.dma_start(wa_raw[b][:], wa_v[:, :, b * PASS : (b + 1) * PASS])
+
+        def load_wd(b, tag):
+            wd_raw.append(staged([P, 4, N], F32, f"wd_raw{b}", tag))
+            rows = wd[b * PASS : (b + 1) * PASS, :].rearrange("(c t v) n -> v c t n", t=4, v=4)
+            for v in range(4):
+                nc.sync.dma_start(wd_raw[b][v:P:4, :, :], rows[v])
+
+        nc.sync.dma_start(tab[:].bitcast(I32), tab_words[0].rearrange("p n t -> p (n t)").bitcast(I32))
+        load_packed(0)
+        load_wa(0, "stage_a")
+        nc.sync.dma_start(idx2[:], offs2)
+
+        g_sc = staged([P, S], U8, "g_sc", "stage_g")
         nc.vector.tensor_copy(g_sc[:], tab_sc[:].indirect(idx[:]))
         planes = kept([P, S + 2 * H], U8, "planes")
         nc.vector.tensor_copy(
@@ -84,60 +89,58 @@ def tile_list_median_codeword_repair_kernel(
         for r in range(1, 4):
             nc.scalar.dma_start(planes[r:P:32, :].bitcast(I32), planes[8 * r : P : 32, :].bitcast(I32))
 
-        load_w(1)
-        wd_raw = []
-
-        def load_wd(b, tag):
-            wd_raw.append(staged([P, 4, N], F32, f"wd_raw{b}", tag))
-            rows = wd[b * PASS : (b + 1) * PASS, :].rearrange("(c t v) n -> v c t n", t=4, v=4)
-            for v in range(4):
-                nc.sync.dma_start(wd_raw[b][v:P:4, :, :], rows[v])
-
-
-        wa16 = [staged([P, 4 * PASS], BF16, "wa16_0", "stage_p2"), kept([P, 4 * PASS], BF16, "wa16_1")]
+        wa16 = [staged([P, 4 * PASS], BF16, "wa16_0", "stage_w"), kept([P, 4 * PASS], BF16, "wa16_1")]
         wa_q = [kept([P, PASS], U32, f"wa_q{b}") for b in range(HB)]
         wa_s = [kept([P, PASS], U8, f"wa_s{b}") for b in range(HB)]
-        wc_q = [kept([P, PASS], I32, f"wc_q{b}") for b in range(HB)]
-        wb_q = [kept([P, PASS // 2], I32, f"wb_q{b}") for b in range(HB)]
+        packed = [staged([P, PASS + PASS // 2], I32, "packed0", "stage_g"), kept([P, PASS + PASS // 2], I32, "packed1")]
+        wc_q = [packed[b][:, 0:PASS] for b in range(HB)]
+        wb_q = [packed[b][:, PASS:] for b in range(HB)]
 
-        def prep_w(b):
-            src = wa_raw[b][:].rearrange("p j (c t v) -> p t c v j", t=4, v=4)
-            dst = wa16[b][:].rearrange("p (t c v j) -> p t c v j", t=4, v=4, j=4)
-            nc.scalar.activation(dst[:, 0], src[:, 0], IDENT)
-            nc.scalar.copy(dst[:, 1:4], src[:, 1:4])
+        def order_packed(b):
             nc.vector.tensor_copy(
-                wc_q[b][:].rearrange("p (t c v) -> p t c v", t=4, v=4),
-                wc_raw[b][:].rearrange("p (c t v) -> p t c v", t=4, v=4),
-            )
-            nc.vector.tensor_copy(
-                wb_q[b][:].rearrange("p (t c v) -> p t c v", t=4, v=2),
+                wb_q[b].rearrange("p (t c v) -> p t c v", t=4, v=2),
                 wb_raw[b][:].rearrange("p (c t v) -> p t c v", t=4, v=2),
             )
+            nc.vector.tensor_copy(
+                wc_q[b].rearrange("p (t c v) -> p t c v", t=4, v=4),
+                wc_raw[b][:].rearrange("p (c t v) -> p t c v", t=4, v=4),
+            )
+
+        def prep_wa(b):
+            src = wa_raw[b][:].rearrange("p j (c t v) -> p t c v j", t=4, v=4)
+            dst = wa16[b][:].rearrange("p (t c v j) -> p t c v j", t=4, v=4, j=4)
+            nc.vector.tensor_copy(dst, src)
             nc.vector.quantize_mx(wa_q[b][:].bitcast(FP8X4), wa_s[b][:], wa16[b][:])
 
-        g_w = kept([P, S], U32, "g_w")
+        g_w = staged([P, S], U32, "g_w", "stage_s")
 
         def gather_words(c):
             nc.vector.tensor_copy(g_w[:, c * CH : (c + 1) * CH], tab[:].indirect(idx[:, c * CH // 16 : (c + 1) * CH // 16]))
 
-        wd16 = [kept([P, 4 * N], BF16, f"wd16_{b}") for b in range(HB)]
+        wd16 = [staged([P, 4 * N], BF16, f"wd16_{b}", f"stage_p{2 + b}") for b in range(HB)]
         wd_q = [kept([P, N], U32, f"wd_q{b}") for b in range(HB)]
         wd_s = [kept([P, N], U8, f"wd_s{b}") for b in range(HB)]
 
         def prep_wd(b):
             src = wd_raw[b][:].rearrange("p t (m i) -> p m i t", i=4)
             dst = wd16[b][:].rearrange("p (i m t) -> p m i t", i=4, t=4)
-            nc.scalar.copy(dst, src)
+            if b == 0:
+                nc.vector.tensor_copy(dst, src)
+            else:
+                nc.scalar.activation(dst, src, IDENT)
             nc.vector.quantize_mx(wd_q[b][:].bitcast(FP8X4), wd_s[b][:], wd16[b][:])
 
         pages = [kept([P, T2], F32, f"page{i}") for i in range(2)]
         pages += [staged([P, T2], F32, f"page{i}", f"stage_p{i}") for i in (2, 3)]
         y = [kept([P, S], F32, f"y{i}") for i in range(4)]
-        h_q = [kept([P, HB, CH], U32, f"h_q{c}") for c in range(NCH)]
-        h_s = [kept([P, HB, CH], U8, f"h_s{c}") for c in range(NCH)]
+        h_q, h_s, h16 = {}, {}, {}
 
-        def estimates(c, b):
-            est = [ring.tile([P, 4 * CH], BF16, name=f"est{w}", align_bytes=64) for w in range(3)]
+        def estimates(c, b, tag=None):
+            if tag is None:
+                three = ring.tile([P, 3 * 4 * CH], BF16, name="est", align_bytes=64)
+            else:
+                three = staged([P, 3 * 4 * CH], BF16, "est_held", tag)
+            est = [three[:, 4 * CH * w : 4 * CH * (w + 1)] for w in range(3)]
             for u in range(CH // UN):
                 j0 = c * CH + u * UN
                 rhs = g_w[:, j0 : j0 + UN].bitcast(FP8X4)
@@ -162,16 +165,23 @@ def tile_list_median_codeword_repair_kernel(
                     )
             return est
 
-        def vote(c, b, est):
+        def quantize_h(c, b, tag):
+            h_q[c, b] = staged([P, CH], U32, f"h_q{c}{b}", tag)
+            h_s[c, b] = kept([P, CH], U8, f"h_s{c}{b}")
+            nc.vector.quantize_mx(h_q[c, b][:].bitcast(FP8X4), h_s[c, b][:], h16[c, b][:])
+
+        def vote(c, b, est, tag=None, behind=None):
+            tag = tag or f"hi{c}{b}"
             lo = ring.tile([P, 4 * CH], BF16, name="lo", align_bytes=64)
-            hi = ring.tile([P, 4 * CH], BF16, name="hi", align_bytes=64)
+            hi = staged([P, 4 * CH], BF16, f"hi{c}{b}", tag)
             mid = ring.tile([P, 4 * CH], BF16, name="mid", align_bytes=64)
-            h16 = ring.tile([P, 4 * CH], BF16, name="h16", align_bytes=64)
-            nc.vector.tensor_tensor(hi[:], est[0][:], est[1][:], ALU.max)
-            nc.vector.tensor_tensor(lo[:], est[0][:], est[1][:], ALU.min)
-            nc.vector.tensor_tensor(mid[:], hi[:], est[2][:], ALU.min)
-            nc.vector.tensor_tensor(h16[:], lo[:], mid[:], ALU.max)
-            nc.vector.quantize_mx(h_q[c][:, b, :].bitcast(FP8X4), h_s[c][:, b, :], h16[:])
+            h16[c, b] = ring.tile([P, 4 * CH], BF16, name="h16", align_bytes=64)
+            nc.vector.tensor_tensor(hi[:], est[0], est[1], ALU.max)
+            nc.vector.tensor_tensor(lo[:], est[0], est[1], ALU.min)
+            nc.vector.tensor_tensor(mid[:], hi[:], est[2], ALU.min)
+            if behind is not None:
+                quantize_h(*behind, tag)
+            nc.vector.tensor_tensor(h16[c, b][:], lo[:], mid[:], ALU.max)
 
         def back(c):
             for half in range(2):
@@ -184,8 +194,8 @@ def tile_list_median_codeword_repair_kernel(
                             bank[:, e, :],
                             lhsT=wd_q[b][:, cols].bitcast(FP8X4),
                             lhsT_scale=wd_s[b][:, cols],
-                            rhs=h_q[c][:, b, :].bitcast(FP8X4),
-                            rhs_scale=h_s[c][:, b, :],
+                            rhs=h_q[c, b][:].bitcast(FP8X4),
+                            rhs_scale=h_s[c, b][:],
                             start=(b == 0),
                             stop=(b == HB - 1),
                         )
@@ -202,33 +212,46 @@ def tile_list_median_codeword_repair_kernel(
 
         out_v = out.rearrange("(p i) t -> p i t", i=4)
 
-        prep_w(0)
-        wa_raw.append(staged([P, 4, PASS], F32, "wa_raw1", "stage_a"))
-        nc.sync.dma_start(wa_raw[1][:], wa_v[:, :, PASS : 2 * PASS])
-        load_wd(0, "stage_c")
-        wgo_sb = staged([P, S], F32, "wgo_sb", "stage_b")
         gather_words(0)
-        est = estimates(0, 0)
-        prep_w(1)
-        load_wd(1, "stage_a")
+        order_packed(0)
+        prep_wa(0)
+        load_wa(1, "stage_b0")
+        load_packed(1)
+        load_wd(0, "stage_a")
+        wgo_sb = staged([P, S], F32, "wgo_sb", "stage_w")
         nc.sync.dma_start(wgo_sb[:], wgo)
-        vote(0, 0, est)
+        est = estimates(0, 0)
         for c in range(1, NCH):
             gather_words(c)
-        est = estimates(0, 1)
-        vote(0, 1, est)
-        for b in range(HB):
-            prep_wd(b)
-        for i in range(4):
+        order_packed(1)
+        prep_wa(1)
+        load_wd(1, "stage_b0")
+        gain = staged([P, 4], F32, "gain", "stage_b1")
+        bias = staged([P, 4], F32, "bias", "stage_c")
+        nc.sync.dma_start(gain[:], gd.rearrange("(p i) -> p i", i=4))
+        nc.sync.dma_start(bias[:], bd.rearrange("(p i) -> p i", i=4))
+        vote(0, 0, est)
+        vote(1, 0, estimates(1, 0), behind=(0, 0))
+        prep_wd(0)
+        vote(0, 1, estimates(0, 1), "stage_a", behind=(1, 0))
+        prep_wd(1)
+        quantize_h(0, 1, "h_q01")
+        vote(1, 1, estimates(1, 1, "stage_b0"))
+        for i in range(2):
             nc.vector.memset(pages[i][:].bitcast(I32), 0)
+        for i in range(2, 4):
+            for q in range(4):
+                nc.gpsimd.memset(pages[i][:, q * T2 // 4 : (q + 1) * T2 // 4].bitcast(I32), 0)
         for c in range(1, NCH + 1):
-            if c < NCH:
-                for b in range(HB):
-                    est = estimates(c, b)
-                    vote(c, b, est)
+            if 1 < c < NCH:
+                vote(c, 1, estimates(c, 1), behind=(c, 0))
             back(c - 1)
             for i in range(3):
                 place(i, (c - 1) * CH, c * CH)
+            if c + 1 < NCH:
+                vote(c + 1, 0, estimates(c + 1, 0), behind=(c, 1))
+            elif c < NCH:
+                quantize_h(c, 1, "h_q_last")
         for i in range(3):
             nc.sync.dma_start(out_v[:, i, :], pages[i][:])
         place(3, 0, S)

@@ -19,9 +19,14 @@ IDENT = mybir.ActivationFunctionType.Identity
 P = 128
 PASS = 512
 HB = H // PASS
-CH = 256
-NCH = S // CH
 UN = 128
+U = 4 * UN
+NJ = S // UN
+FIRST = 256
+LEAD = 3
+REGIONS = 6
+KB = 1024
+LO, X1, MID, X2, HH, HI, X0 = range(7)
 
 
 def tile_list_median_codeword_repair_kernel(
@@ -30,229 +35,229 @@ def tile_list_median_codeword_repair_kernel(
     nc = tc.nc
     with ExitStack() as ctx:
         keep = ctx.enter_context(tc.tile_pool(name="keep", bufs=1))
-        ring = ctx.enter_context(tc.tile_pool(name="ring", bufs=3))
-        psum = ctx.enter_context(tc.psum_pool(name="psum", bufs=2))
+        stage = ctx.enter_context(tc.tile_pool(name="stage", bufs=1))
+        psum = ctx.enter_context(tc.psum_pool(name="psum", bufs=1))
 
-        def kept(shape, dtype, name):
-            return keep.tile(shape, dtype, name=name, align_bytes=64)
+        def kept(shape, dtype, name, tag=None):
+            return keep.tile(shape, dtype, name=name, tag=tag or name, align_bytes=64)
 
-        def staged(shape, dtype, name, tag):
-            return keep.tile(shape, dtype, name=name, tag=tag, align_bytes=64)
+        def placed(shape, dtype, name, offset):
+            return stage.tile(shape, dtype, name=name, offset=offset, align_bytes=64)
 
         idx = kept([P, S // 16], U16, "idx")
         idx2 = kept([P, S // 16], U16, "idx2")
         nc.sync.dma_start(idx[:], offs)
 
-        tab_sc = staged([P, T], U8, "tab_sc", "stage_s")
-        w_sc = staged([P, 2 * H], U8, "w_sc", "stage_w")
-        nc.vector.memset(tab_sc[:].bitcast(I32), 0)
-        nc.gpsimd.memset(w_sc[:].bitcast(I32), 0)
-        nc.scalar.dma_start(tab_sc[0:P:8, :].bitcast(I32), tab_scales[0].bitcast(I32))
-        nc.scalar.dma_start(w_sc[0:P:8, 0:H].bitcast(I32), wb_scales[0].bitcast(I32))
-        nc.scalar.dma_start(w_sc[0:P:8, H : 2 * H].bitcast(I32), wc_scales[0].bitcast(I32))
+        tab_sc = placed([P, T], U8, "tab_sc", 3 * KB)
+        w_sc = kept([P, 2 * H], U8, "w_sc")
+        nc.scalar.dma_start(tab_sc[:].bitcast(I32), tab_scales[0].bitcast(I32).unsqueeze(1).to_broadcast([16, 8, T // 4]))
+        nc.sync.dma_start(w_sc[:, 0:H].bitcast(I32), wb_scales[0].bitcast(I32).unsqueeze(1).to_broadcast([16, 8, H // 4]))
+        nc.scalar.dma_start(w_sc[:, H : 2 * H].bitcast(I32), wc_scales[0].bitcast(I32).unsqueeze(1).to_broadcast([16, 8, H // 4]))
 
-        tab = kept([P, T], U32, "tab")
-        wa_v = wa.rearrange("(p j) c -> p j c", j=4)
-        wc_v = wc_words[0].rearrange("p n t -> p (n t)").bitcast(I32)
-        wb_v = wb_words[0].bitcast(I32)
-        wa_raw, wb_raw, wc_raw, wd_raw = [], [], [], []
-
-        def load_packed(b):
-            wb_raw.append(staged([P, PASS // 2], I32, f"wb_raw{b}", f"stage_b{b}"))
-            wc_raw.append(staged([P, PASS], I32, f"wc_raw{b}", "stage_c"))
-            nc.sync.dma_start(wb_raw[b][:], wb_v[:, b * PASS // 2 : (b + 1) * PASS // 2])
-            nc.sync.dma_start(wc_raw[b][:], wc_v[:, b * PASS : (b + 1) * PASS])
-
-        def load_wa(b, tag):
-            wa_raw.append(staged([P, 4, PASS], F32, f"wa_raw{b}", tag))
-            nc.sync.dma_start(wa_raw[b][:], wa_v[:, :, b * PASS : (b + 1) * PASS])
-
-        def load_wd(b, tag):
-            wd_raw.append(staged([P, 4, N], F32, f"wd_raw{b}", tag))
-            rows = wd[b * PASS : (b + 1) * PASS, :].rearrange("(c t v) n -> v c t n", t=4, v=4)
-            for v in range(4):
-                nc.sync.dma_start(wd_raw[b][v:P:4, :, :], rows[v])
-
-        nc.sync.dma_start(tab[:].bitcast(I32), tab_words[0].rearrange("p n t -> p (n t)").bitcast(I32))
-        load_packed(0)
-        load_wa(0, "stage_a")
         nc.sync.dma_start(idx2[:], offs2)
 
-        g_sc = staged([P, S], U8, "g_sc", "stage_g")
+        wa_v = wa.rearrange("(p j) c -> p j c", j=4)
+        wa_raw0 = placed([P, 4 * PASS], F32, "wa_raw0", 16 * KB)
+        tab = kept([P, T], U32, "tab")
+        wb_raw = kept([P, H // 2], I32, "wb_raw", "raw_b")
+        wc_raw = kept([P, H], I32, "wc_raw", "raw_c")
+        nc.scalar.dma_start(wa_raw0[:].rearrange("p (j c) -> p j c", j=4), wa_v[:, :, 0:PASS])
+        nc.scalar.dma_start(tab[:].bitcast(I32), tab_words[0].rearrange("p n t -> p (n t)").bitcast(I32))
+        nc.scalar.dma_start(wb_raw[:], wb_words[0].bitcast(I32))
+        nc.scalar.dma_start(wc_raw[:], wc_words[0].rearrange("p n t -> p (n t)").bitcast(I32))
+
+        pages = [kept([P, T2], F32, f"page{i}") for i in range(2)]
+
+        g_sc = placed([P, S], U8, "g_sc", 15 * KB // 2)
         nc.vector.tensor_copy(g_sc[:], tab_sc[:].indirect(idx[:]))
         planes = kept([P, S + 2 * H], U8, "planes")
+        nc.vector.tensor_copy(planes[:, 0:S].bitcast(I32), g_sc[:].bitcast(I32))
         nc.vector.tensor_copy(
             planes[:, S:].bitcast(I32).rearrange("p (a t c) -> p a t c", t=4, c=32),
             w_sc[:].bitcast(I32).rearrange("p (a c t) -> p a t c", t=4, c=32),
         )
-        nc.vector.tensor_copy(planes[:, 0:S].bitcast(I32), g_sc[:].bitcast(I32))
         for r in range(1, 4):
-            nc.scalar.dma_start(planes[r:P:32, :].bitcast(I32), planes[8 * r : P : 32, :].bitcast(I32))
+            nc.sync.dma_start(planes[r:P:32, :].bitcast(I32), planes[8 * r : P : 32, :].bitcast(I32))
 
-        wa16 = [staged([P, 4 * PASS], BF16, "wa16_0", "stage_w"), kept([P, 4 * PASS], BF16, "wa16_1")]
-        wa_q = [kept([P, PASS], U32, f"wa_q{b}") for b in range(HB)]
-        wa_s = [kept([P, PASS], U8, f"wa_s{b}") for b in range(HB)]
-        packed = [staged([P, PASS + PASS // 2], I32, "packed0", "stage_g"), kept([P, PASS + PASS // 2], I32, "packed1")]
-        wc_q = [packed[b][:, 0:PASS] for b in range(HB)]
-        wb_q = [packed[b][:, PASS:] for b in range(HB)]
+        wa_raw1 = placed([P, 4 * PASS], F32, "wa_raw1", 12 * KB)
+        wd_raw = placed([P, HB * 4 * N], F32, "wd_raw", 20 * KB)
+        wd_raw0, wd_raw1 = wd_raw[:, 0 : 4 * N], wd_raw[:, 4 * N :]
+        nc.sync.dma_start(wa_raw1[:].rearrange("p (j c) -> p j c", j=4), wa_v[:, :, PASS:])
 
-        def order_packed(b):
-            nc.vector.tensor_copy(
-                wb_q[b].rearrange("p (t c v) -> p t c v", t=4, v=2),
-                wb_raw[b][:].rearrange("p (c t v) -> p t c v", t=4, v=2),
-            )
-            nc.vector.tensor_copy(
-                wc_q[b].rearrange("p (t c v) -> p t c v", t=4, v=4),
-                wc_raw[b][:].rearrange("p (c t v) -> p t c v", t=4, v=4),
-            )
+        def load_wd(b, raw):
+            rows = wd[b * PASS : (b + 1) * PASS, :].rearrange("(c t v) n -> t c (v n)", t=4, v=4)
+            for t in range(4):
+                nc.sync.dma_start(raw[:, t * N : (t + 1) * N], rows[t])
 
-        def prep_wa(b):
-            src = wa_raw[b][:].rearrange("p j (c t v) -> p t c v j", t=4, v=4)
-            dst = wa16[b][:].rearrange("p (t c v j) -> p t c v j", t=4, v=4, j=4)
-            nc.vector.tensor_copy(dst, src)
-            nc.vector.quantize_mx(wa_q[b][:].bitcast(FP8X4), wa_s[b][:], wa16[b][:])
+        load_wd(0, wd_raw0)
+        load_wd(1, wd_raw1)
 
-        g_w = staged([P, S], U32, "g_w", "stage_s")
+        def quantised(name, width):
+            return kept([P, width], U32, name + "_q"), kept([P, width], U8, name + "_s")
 
-        def gather_words(c):
-            nc.vector.tensor_copy(g_w[:, c * CH : (c + 1) * CH], tab[:].indirect(idx[:, c * CH // 16 : (c + 1) * CH // 16]))
+        def cast_wa(copy, raw, name):
+            w16 = kept([P, 4 * PASS], BF16, name)
+            copy(w16[:].rearrange("p (t c v j) -> p t c v j", t=4, v=4, j=4), raw[:].rearrange("p (j c t v) -> p t c v j", j=4, t=4, v=4))
+            return w16
 
-        wd16 = [staged([P, 4 * N], BF16, f"wd16_{b}", f"stage_p{2 + b}") for b in range(HB)]
-        wd_q = [kept([P, N], U32, f"wd_q{b}") for b in range(HB)]
-        wd_s = [kept([P, N], U8, f"wd_s{b}") for b in range(HB)]
+        def cast_wd(copy, raw, name, offset):
+            w16 = placed([P, 4 * N], BF16, name, offset)
+            copy(w16[:].rearrange("p (i m t) -> p m i t", i=4, t=4), raw.rearrange("p (t m i) -> p m i t", t=4, i=4))
+            return w16
 
-        def prep_wd(b):
-            src = wd_raw[b][:].rearrange("p t (m i) -> p m i t", i=4)
-            dst = wd16[b][:].rearrange("p (i m t) -> p m i t", i=4, t=4)
-            if b == 0:
-                nc.vector.tensor_copy(dst, src)
-            else:
-                nc.scalar.activation(dst, src, IDENT)
-            nc.vector.quantize_mx(wd_q[b][:].bitcast(FP8X4), wd_s[b][:], wd16[b][:])
+        def quantise(qs, w16):
+            nc.vector.quantize_mx(qs[0].bitcast(FP8X4), qs[1], w16)
 
-        pages = [kept([P, T2], F32, f"page{i}") for i in range(2)]
-        pages += [staged([P, T2], F32, f"page{i}", f"stage_p{i}") for i in (2, 3)]
+        wa_qs = [(placed([P, PASS], U32, "wa0_q", 4 * KB), kept([P, PASS], U8, "wa0_s")), quantised("wa1", PASS)]
+        wd_qs = [quantised(f"wd{b}", N) for b in range(HB)]
+        h_qs = [quantised(f"h{b}", S) for b in range(HB)]
+
+        wa16_0 = cast_wa(nc.scalar.copy, wa_raw0, "wa16_0")
+
+
+        g_w = placed([P, S], U32, "g_w", 0)
+        nc.vector.tensor_copy(g_w[:, 0:FIRST], tab[:].indirect(idx[:, 0 : FIRST // 16]))
+        wb_q = placed([P, H // 2], I32, "wb_q", 6 * KB)
+        wc_q = placed([P, H], I32, "wc_q", 8 * KB)
+        nc.vector.tensor_copy(
+            wb_q[:].rearrange("p (b t c v) -> p b t c v", b=HB, t=4, v=2),
+            wb_raw[:].rearrange("p (b c t v) -> p b t c v", b=HB, t=4, v=2),
+        )
+        nc.vector.tensor_copy(
+            wc_q[:].rearrange("p (b t c v) -> p b t c v", b=HB, t=4, v=4),
+            wc_raw[:].rearrange("p (b c t v) -> p b t c v", b=HB, t=4, v=4),
+        )
+        quantise([x[:] for x in wa_qs[0]], wa16_0[:])
+        nc.vector.tensor_copy(g_w[:, FIRST:], tab[:].indirect(idx[:, FIRST // 16 :]))
+
+        wa16_1 = cast_wa(nc.vector.tensor_copy, wa_raw1, "wa16_1")
+
+        wgo_sb = placed([P, S], F32, "wgo_sb", 12 * KB)
+        nc.sync.dma_start(wgo_sb[:], wgo)
+        affine = placed([P, 16], F32, "affine", 16 * KB)
+        nc.sync.dma_start(affine[:, 0:4], gd.rearrange("(p i) -> p i", i=4))
+        nc.sync.dma_start(affine[:, 8:12], bd.rearrange("(p i) -> p i", i=4))
+
+        for i in range(2):
+            for q in range(2):
+                nc.vector.memset(pages[i][:, q * T2 // 2 : (q + 1) * T2 // 2].bitcast(I32), 0)
+
+        est_banks = [psum.tile([P, 4, UN], F32, name=f"est_bank{e}") for e in range(6)]
+        y_banks = [psum.tile([P, PASS], F32, name=f"y_bank{e}") for e in range(2)]
+        regions = [kept([P, 7 * U], BF16, f"region{e}") for e in range(LEAD)]
+        regions += [placed([P, 7 * U], BF16, f"region{LEAD + e}", (20 + 8 * e) * KB) for e in range(2)]
+        regions += [kept([P, 7 * U], BF16, f"region{e}") for e in range(LEAD + 2, REGIONS)]
         y = [kept([P, S], F32, f"y{i}") for i in range(4)]
-        h_q, h_s, h16 = {}, {}, {}
 
-        def estimates(c, b, tag=None):
-            if tag is None:
-                three = ring.tile([P, 3 * 4 * CH], BF16, name="est", align_bytes=64)
+        def slot(k, first, count=1):
+            return regions[k % REGIONS][:, first * U : (first + count) * U]
+
+        units = [(j, 0) for j in range(LEAD)] + [(j, 1) for j in range(LEAD)]
+        units += [(j, b) for j in range(LEAD, NJ) for b in range(HB)]
+
+        def estimates(k):
+            j, b = units[k]
+            rhs = g_w[:, j * UN : (j + 1) * UN].bitcast(FP8X4)
+            rhs_s = planes[:, j * UN : (j + 1) * UN]
+            order = (X1, X2, X0) if k == 0 else (X0, X1, X2)
+            for e, x in enumerate(order):
+                bank = est_banks[3 * (k % 2) + e]
+                for t in range(4):
+                    c0 = b * PASS + t * P
+                    if x == X1:
+                        lhs = wb_q[:, c0 // 2 : (c0 + P) // 2].bitcast(FP4X4)
+                        lhs_s = planes[:, S + c0 : S + c0 + P]
+                    elif x == X2:
+                        lhs = wc_q[:, c0 : c0 + P].bitcast(FP8X4)
+                        lhs_s = planes[:, S + H + c0 : S + H + c0 + P]
+                    else:
+                        lhs = wa_qs[b][0][:, t * P : (t + 1) * P].bitcast(FP8X4)
+                        lhs_s = wa_qs[b][1][:, t * P : (t + 1) * P]
+                    nc.tensor.matmul_mx(bank[:, t, :], lhsT=lhs, lhsT_scale=lhs_s, rhs=rhs, rhs_scale=rhs_s, start=True, stop=True)
+                nc.scalar.copy(slot(k, x).rearrange("p (n t) -> p n t", t=4), bank[:].rearrange("p t n -> p n t"))
+
+        def quantise_h(k):
+            j, b = units[k]
+            quantise([x[:, j * UN : (j + 1) * UN] for x in h_qs[b]], slot(k + 1, HH))
+
+        def vote(k):
+            if k == 0:
+                nc.vector.tensor_tensor(slot(k, HI), slot(k, X1), slot(k, X2), ALU.max)
             else:
-                three = staged([P, 3 * 4 * CH], BF16, "est_held", tag)
-            est = [three[:, 4 * CH * w : 4 * CH * (w + 1)] for w in range(3)]
-            for u in range(CH // UN):
-                j0 = c * CH + u * UN
-                rhs = g_w[:, j0 : j0 + UN].bitcast(FP8X4)
-                rhs_s = planes[:, j0 : j0 + UN]
-                for w in range(3):
-                    bank = psum.tile([P, 4, UN], F32, name=f"bank{w}")
-                    for t in range(4):
-                        cols = slice(t * P, (t + 1) * P)
-                        if w == 0:
-                            lhs = wb_q[b][:, t * P // 2 : (t + 1) * P // 2].bitcast(FP4X4)
-                            lhs_s = planes[:, S + b * PASS + t * P : S + b * PASS + (t + 1) * P]
-                        elif w == 1:
-                            lhs = wc_q[b][:, cols].bitcast(FP8X4)
-                            lhs_s = planes[:, S + H + b * PASS + t * P : S + H + b * PASS + (t + 1) * P]
-                        else:
-                            lhs = wa_q[b][:, cols].bitcast(FP8X4)
-                            lhs_s = wa_s[b][:, cols]
-                        nc.tensor.matmul_mx(bank[:, t, :], lhsT=lhs, lhsT_scale=lhs_s, rhs=rhs, rhs_scale=rhs_s, start=True, stop=True)
-                    nc.scalar.copy(
-                        est[w][:, 4 * u * UN : 4 * (u + 1) * UN].rearrange("p (n t) -> p n t", t=4),
-                        bank[:].rearrange("p t n -> p n t"),
-                    )
-            return est
+                nc.vector.tensor_tensor(slot(k, HH, 2), slot(k, LO, 2), slot(k, MID, 2), ALU.max)
+            nc.vector.tensor_tensor(slot(k + 1, LO), slot(k, X1), slot(k, X2), ALU.min)
+            nc.vector.tensor_tensor(slot(k + 1, MID), slot(k, HI), slot(k, X0), ALU.min)
+            if k > 0:
+                quantise_h(k - 1)
 
-        def quantize_h(c, b, tag):
-            h_q[c, b] = staged([P, CH], U32, f"h_q{c}{b}", tag)
-            h_s[c, b] = kept([P, CH], U8, f"h_s{c}{b}")
-            nc.vector.quantize_mx(h_q[c, b][:].bitcast(FP8X4), h_s[c, b][:], h16[c, b][:])
+        made = []
 
-        def vote(c, b, est, tag=None, behind=None):
-            tag = tag or f"hi{c}{b}"
-            lo = ring.tile([P, 4 * CH], BF16, name="lo", align_bytes=64)
-            hi = staged([P, 4 * CH], BF16, f"hi{c}{b}", tag)
-            mid = ring.tile([P, 4 * CH], BF16, name="mid", align_bytes=64)
-            h16[c, b] = ring.tile([P, 4 * CH], BF16, name="h16", align_bytes=64)
-            nc.vector.tensor_tensor(hi[:], est[0], est[1], ALU.max)
-            nc.vector.tensor_tensor(lo[:], est[0], est[1], ALU.min)
-            nc.vector.tensor_tensor(mid[:], hi[:], est[2], ALU.min)
-            if behind is not None:
-                quantize_h(*behind, tag)
-            nc.vector.tensor_tensor(h16[c, b][:], lo[:], mid[:], ALU.max)
-
-        def back(c):
-            for half in range(2):
-                bank = psum.tile([P, 2, CH], F32, name="bank_y")
-                for e in range(2):
-                    i = 2 * half + e
-                    cols = slice(i * P, (i + 1) * P)
-                    for b in range(HB):
-                        nc.tensor.matmul_mx(
-                            bank[:, e, :],
-                            lhsT=wd_q[b][:, cols].bitcast(FP8X4),
-                            lhsT_scale=wd_s[b][:, cols],
-                            rhs=h_q[c, b][:].bitcast(FP8X4),
-                            rhs_scale=h_s[c, b][:],
-                            start=(b == 0),
-                            stop=(b == HB - 1),
-                        )
-                for e in range(2):
-                    i = 2 * half + e
-                    nc.scalar.activation(
-                        y[i][:, c * CH : (c + 1) * CH], bank[:, e, :], IDENT, bias=bias[:, i : i + 1], scale=gain[:, i : i + 1]
-                    )
+        def back(i, j0, j1):
+            bank = y_banks[len(made) % 2]
+            made.append(i)
+            for b in range(HB):
+                nc.tensor.matmul_mx(
+                    bank[:, 0 : j1 - j0],
+                    lhsT=wd_qs[b][0][:, i * P : (i + 1) * P].bitcast(FP8X4),
+                    lhsT_scale=wd_qs[b][1][:, i * P : (i + 1) * P],
+                    rhs=h_qs[b][0][:, j0:j1].bitcast(FP8X4),
+                    rhs_scale=h_qs[b][1][:, j0:j1],
+                    start=(b == 0),
+                    stop=(b == HB - 1),
+                )
+            nc.scalar.activation(y[i][:, j0:j1], bank[:, 0 : j1 - j0], IDENT, bias=affine[:, 8 + i : 9 + i], scale=affine[:, i : i + 1])
 
         def place(i, j0, j1):
-            nc.vector.tensor_tensor(
-                pages[i][:].indirect(idx2[:, j0 // 16 : j1 // 16]), y[i][:, j0:j1], wgo_sb[:, j0:j1], ALU.mult
-            )
+            nc.vector.tensor_tensor(pages[i][:].indirect(idx2[:, j0 // 16 : j1 // 16]), y[i][:, j0:j1], wgo_sb[:, j0:j1], ALU.mult)
 
-        out_v = out.rearrange("(p i) t -> p i t", i=4)
-
-        gather_words(0)
-        order_packed(0)
-        prep_wa(0)
-        load_wa(1, "stage_b0")
-        load_packed(1)
-        load_wd(0, "stage_a")
-        wgo_sb = staged([P, S], F32, "wgo_sb", "stage_w")
-        nc.sync.dma_start(wgo_sb[:], wgo)
-        est = estimates(0, 0)
-        for c in range(1, NCH):
-            gather_words(c)
-        order_packed(1)
-        prep_wa(1)
-        load_wd(1, "stage_b0")
-        gain = staged([P, 4], F32, "gain", "stage_b1")
-        bias = staged([P, 4], F32, "bias", "stage_c")
-        nc.sync.dma_start(gain[:], gd.rearrange("(p i) -> p i", i=4))
-        nc.sync.dma_start(bias[:], bd.rearrange("(p i) -> p i", i=4))
-        vote(0, 0, est)
-        vote(1, 0, estimates(1, 0), behind=(0, 0))
-        prep_wd(0)
-        vote(0, 1, estimates(0, 1), "stage_a", behind=(1, 0))
-        prep_wd(1)
-        quantize_h(0, 1, "h_q01")
-        vote(1, 1, estimates(1, 1, "stage_b0"))
-        for i in range(2):
-            nc.vector.memset(pages[i][:].bitcast(I32), 0)
-        for i in range(2, 4):
+        def clear_page(i, offset):
+            pages.append(placed([P, T2], F32, f"page{i}", offset))
             for q in range(4):
                 nc.gpsimd.memset(pages[i][:, q * T2 // 4 : (q + 1) * T2 // 4].bitcast(I32), 0)
-        for c in range(1, NCH + 1):
-            if 1 < c < NCH:
-                vote(c, 1, estimates(c, 1), behind=(c, 0))
-            back(c - 1)
-            for i in range(3):
-                place(i, (c - 1) * CH, c * CH)
-            if c + 1 < NCH:
-                vote(c + 1, 0, estimates(c + 1, 0), behind=(c, 1))
-            elif c < NCH:
-                quantize_h(c, 1, "h_q_last")
-        for i in range(3):
+
+        out_v = out.rearrange("(p i) t -> p i t", i=4)
+        ready = []
+        last = len(units) - 1
+        for k in range(len(units)):
+            estimates(k)
+            if k == LEAD - 1:
+                wd16_0 = cast_wd(nc.scalar.copy, wd_raw0, "wd16_0", 36 * KB)
+                wd16_1 = cast_wd(nc.vector.tensor_copy, wd_raw1, "wd16_1", 40 * KB)
+            piece = ready.pop(0) if ready else None
+            if piece:
+                back(*piece)
+            vote(k)
+            if piece:
+                place(*piece)
+            if k > 0 and units[k - 1][1] == 1:
+                j = units[k - 1][0]
+                ready += [(i, j * UN, (j + 1) * UN) for i in range(2)]
+            if k == 0:
+                quantise([x[:] for x in wa_qs[1]], wa16_1[:])
+            if k == LEAD - 1:
+                quantise([x[:] for x in wd_qs[0]], wd16_0[:])
+                quantise([x[:] for x in wd_qs[1]], wd16_1[:])
+                clear_page(2, 36 * KB)
+
+        clear_page(3, 0)
+        for piece in ready:
+            back(*piece)
+        place(*ready.pop(0))
+        nc.vector.tensor_tensor(slot(last + 1, HH), slot(last + 1, LO), slot(last + 1, MID), ALU.max)
+        place(*ready.pop(0))
+        quantise_h(last)
+        for piece in ready:
+            place(*piece)
+        back(2, 0, PASS)
+        place(2, 0, PASS)
+        for i in range(2):
+            back(i, S - UN, S)
+            place(i, S - UN, S)
             nc.sync.dma_start(out_v[:, i, :], pages[i][:])
+        back(2, PASS, S)
+        place(2, PASS, S)
+        nc.sync.dma_start(out_v[:, 2, :], pages[2][:])
+        back(3, 0, PASS)
+        back(3, PASS, S)
         place(3, 0, S)
         nc.sync.dma_start(out_v[:, 3, :], pages[3][:])

@@ -20,13 +20,13 @@ P = 128
 PASS = 512
 HB = H // PASS
 UN = 128
-U = 4 * UN
-NJ = S // UN
+WIDE = 2 * UN
 FIRST = 256
 LEAD = 3
-REGIONS = 6
+REGIONS = 7
+CLEAR3 = 8
+SPLIT2 = 640
 KB = 1024
-LO, X1, MID, X2, HH, HI, X0 = range(7)
 
 
 def tile_list_median_codeword_repair_kernel(
@@ -62,11 +62,13 @@ def tile_list_median_codeword_repair_kernel(
         wb_raw = kept([P, H // 2], I32, "wb_raw", "raw_b")
         wc_raw = kept([P, H], I32, "wc_raw", "raw_c")
         nc.scalar.dma_start(wa_raw0[:].rearrange("p (j c) -> p j c", j=4), wa_v[:, :, 0:PASS])
+        wa_raw1 = placed([P, 4 * PASS], F32, "wa_raw1", 72 * KB)
+        nc.scalar.dma_start(wa_raw1[:].rearrange("p (j c) -> p j c", j=4), wa_v[:, :, PASS:])
         nc.scalar.dma_start(tab[:].bitcast(I32), tab_words[0].rearrange("p n t -> p (n t)").bitcast(I32))
         nc.scalar.dma_start(wb_raw[:], wb_words[0].bitcast(I32))
         nc.scalar.dma_start(wc_raw[:], wc_words[0].rearrange("p n t -> p (n t)").bitcast(I32))
 
-        pages = [kept([P, T2], F32, f"page{i}") for i in range(2)]
+        pages = [kept([P, T2], F32, f"page{i}") for i in range(3)]
 
         g_sc = placed([P, S], U8, "g_sc", 15 * KB // 2)
         nc.vector.tensor_copy(g_sc[:], tab_sc[:].indirect(idx[:]))
@@ -79,10 +81,8 @@ def tile_list_median_codeword_repair_kernel(
         for r in range(1, 4):
             nc.sync.dma_start(planes[r:P:32, :].bitcast(I32), planes[8 * r : P : 32, :].bitcast(I32))
 
-        wa_raw1 = placed([P, 4 * PASS], F32, "wa_raw1", 12 * KB)
         wd_raw = placed([P, HB * 4 * N], F32, "wd_raw", 20 * KB)
         wd_raw0, wd_raw1 = wd_raw[:, 0 : 4 * N], wd_raw[:, 4 * N :]
-        nc.sync.dma_start(wa_raw1[:].rearrange("p (j c) -> p j c", j=4), wa_v[:, :, PASS:])
 
         def load_wd(b, raw):
             rows = wd[b * PASS : (b + 1) * PASS, :].rearrange("(c t v) n -> t c (v n)", t=4, v=4)
@@ -113,6 +113,7 @@ def tile_list_median_codeword_repair_kernel(
         h_qs = [quantised(f"h{b}", S) for b in range(HB)]
 
         wa16_0 = cast_wa(nc.scalar.copy, wa_raw0, "wa16_0")
+        wa16_1 = cast_wa(nc.scalar.copy, wa_raw1, "wa16_1")
 
 
         g_w = placed([P, S], U32, "g_w", 0)
@@ -128,65 +129,76 @@ def tile_list_median_codeword_repair_kernel(
             wc_raw[:].rearrange("p (b c t v) -> p b t c v", b=HB, t=4, v=4),
         )
         quantise([x[:] for x in wa_qs[0]], wa16_0[:])
+        quantise([x[:] for x in wa_qs[1]], wa16_1[:])
         nc.vector.tensor_copy(g_w[:, FIRST:], tab[:].indirect(idx[:, FIRST // 16 :]))
 
-        wa16_1 = cast_wa(nc.vector.tensor_copy, wa_raw1, "wa16_1")
 
-        wgo_sb = placed([P, S], F32, "wgo_sb", 12 * KB)
+        wgo_sb = placed([P, S], F32, "wgo_sb", 72 * KB)
         nc.sync.dma_start(wgo_sb[:], wgo)
-        affine = placed([P, 16], F32, "affine", 16 * KB)
+        affine = placed([P, 16], F32, "affine", 76 * KB)
         nc.sync.dma_start(affine[:, 0:4], gd.rearrange("(p i) -> p i", i=4))
         nc.sync.dma_start(affine[:, 8:12], bd.rearrange("(p i) -> p i", i=4))
 
-        for i in range(2):
+        for i in range(3):
             for q in range(2):
                 nc.vector.memset(pages[i][:, q * T2 // 2 : (q + 1) * T2 // 2].bitcast(I32), 0)
 
         est_banks = [psum.tile([P, 4, UN], F32, name=f"est_bank{e}") for e in range(6)]
         y_banks = [psum.tile([P, PASS], F32, name=f"y_bank{e}") for e in range(2)]
-        regions = [kept([P, 7 * U], BF16, f"region{e}") for e in range(LEAD)]
-        regions += [placed([P, 7 * U], BF16, f"region{LEAD + e}", (20 + 8 * e) * KB) for e in range(2)]
-        regions += [kept([P, 7 * U], BF16, f"region{e}") for e in range(LEAD + 2, REGIONS)]
+        spans = [(j * UN, (j + 1) * UN) for j in range(LEAD)]
+        units = [(j0, j1, b) for j0, j1 in spans for b in range(HB)]
+        spans = [(j0, j0 + WIDE) for j0 in range(LEAD * UN, S - UN, WIDE)] + [(S - UN, S)]
+        units += [(j0, j1, b) for j0, j1 in spans for b in range(HB)]
+        last = len(units) - 1
+
+        size = 7 * 4 * WIDE
+        regions = [kept([P, size], BF16, "region0"), placed([P, size], BF16, "region1", 58 * KB), kept([P, size], BF16, "region2")]
+        regions += [placed([P, size], BF16, f"region{LEAD}", 20 * KB), placed([P, size], BF16, f"region{LEAD + 1}", 34 * KB)]
+        regions += [kept([P, size], BF16, f"region{e}") for e in range(LEAD + 2, REGIONS)]
         y = [kept([P, S], F32, f"y{i}") for i in range(4)]
 
-        def slot(k, first, count=1):
-            return regions[k % REGIONS][:, first * U : (first + count) * U]
+        def slot(k, first, end=None):
+            before = 4 * (units[k - 1][1] - units[k - 1][0]) if k > 0 else 0
+            own = 4 * (units[k][1] - units[k][0]) if k <= last else 0
+            widths = [before, own, before, own, before, own, own]
+            names = ["lo", "x1", "mid", "x2", "h", "hi", "x0"]
+            a, z = names.index(first), names.index(end or first)
+            return regions[k % REGIONS][:, sum(widths[:a]) : sum(widths[: z + 1])]
 
-        units = [(j, 0) for j in range(LEAD)] + [(j, 1) for j in range(LEAD)]
-        units += [(j, b) for j in range(LEAD, NJ) for b in range(HB)]
+        filled = []
 
         def estimates(k):
-            j, b = units[k]
-            rhs = g_w[:, j * UN : (j + 1) * UN].bitcast(FP8X4)
-            rhs_s = planes[:, j * UN : (j + 1) * UN]
-            order = (X1, X2, X0) if k == 0 else (X0, X1, X2)
-            for e, x in enumerate(order):
-                bank = est_banks[3 * (k % 2) + e]
-                for t in range(4):
-                    c0 = b * PASS + t * P
-                    if x == X1:
-                        lhs = wb_q[:, c0 // 2 : (c0 + P) // 2].bitcast(FP4X4)
-                        lhs_s = planes[:, S + c0 : S + c0 + P]
-                    elif x == X2:
-                        lhs = wc_q[:, c0 : c0 + P].bitcast(FP8X4)
-                        lhs_s = planes[:, S + H + c0 : S + H + c0 + P]
-                    else:
-                        lhs = wa_qs[b][0][:, t * P : (t + 1) * P].bitcast(FP8X4)
-                        lhs_s = wa_qs[b][1][:, t * P : (t + 1) * P]
-                    nc.tensor.matmul_mx(bank[:, t, :], lhsT=lhs, lhsT_scale=lhs_s, rhs=rhs, rhs_scale=rhs_s, start=True, stop=True)
-                nc.scalar.copy(slot(k, x).rearrange("p (n t) -> p n t", t=4), bank[:].rearrange("p t n -> p n t"))
+            j0, j1, b = units[k]
+            order = ("x1", "x2", "x0") if k == 0 else ("x0", "x1", "x2")
+            for j in range(j0, j1, UN):
+                rhs = g_w[:, j : j + UN].bitcast(FP8X4)
+                rhs_s = planes[:, j : j + UN]
+                for x in order:
+                    bank = est_banks[len(filled) % len(est_banks)]
+                    filled.append(x)
+                    for t in range(4):
+                        c0 = b * PASS + t * P
+                        if x == "x1":
+                            lhs = wb_q[:, c0 // 2 : (c0 + P) // 2].bitcast(FP4X4)
+                            lhs_s = planes[:, S + c0 : S + c0 + P]
+                        elif x == "x2":
+                            lhs = wc_q[:, c0 : c0 + P].bitcast(FP8X4)
+                            lhs_s = planes[:, S + H + c0 : S + H + c0 + P]
+                        else:
+                            lhs = wa_qs[b][0][:, t * P : (t + 1) * P].bitcast(FP8X4)
+                            lhs_s = wa_qs[b][1][:, t * P : (t + 1) * P]
+                        nc.tensor.matmul_mx(bank[:, t, :], lhsT=lhs, lhsT_scale=lhs_s, rhs=rhs, rhs_scale=rhs_s, start=True, stop=True)
+                    into = slot(k, x)[:, 4 * (j - j0) : 4 * (j - j0 + UN)]
+                    nc.scalar.copy(into.rearrange("p (n t) -> p n t", t=4), bank[:].rearrange("p t n -> p n t"))
 
         def quantise_h(k):
-            j, b = units[k]
-            quantise([x[:, j * UN : (j + 1) * UN] for x in h_qs[b]], slot(k + 1, HH))
+            j0, j1, b = units[k]
+            quantise([x[:, j0:j1] for x in h_qs[b]], slot(k + 1, "h"))
 
         def vote(k):
-            if k == 0:
-                nc.vector.tensor_tensor(slot(k, HI), slot(k, X1), slot(k, X2), ALU.max)
-            else:
-                nc.vector.tensor_tensor(slot(k, HH, 2), slot(k, LO, 2), slot(k, MID, 2), ALU.max)
-            nc.vector.tensor_tensor(slot(k + 1, LO), slot(k, X1), slot(k, X2), ALU.min)
-            nc.vector.tensor_tensor(slot(k + 1, MID), slot(k, HI), slot(k, X0), ALU.min)
+            nc.vector.tensor_tensor(slot(k, "h", "hi"), slot(k, "lo", "x1"), slot(k, "mid", "x2"), ALU.max)
+            nc.vector.tensor_tensor(slot(k + 1, "lo"), slot(k, "x1"), slot(k, "x2"), ALU.min)
+            nc.vector.tensor_tensor(slot(k + 1, "mid"), slot(k, "hi"), slot(k, "x0"), ALU.min)
             if k > 0:
                 quantise_h(k - 1)
 
@@ -217,47 +229,42 @@ def tile_list_median_codeword_repair_kernel(
 
         out_v = out.rearrange("(p i) t -> p i t", i=4)
         ready = []
-        last = len(units) - 1
         for k in range(len(units)):
             estimates(k)
-            if k == LEAD - 1:
-                wd16_0 = cast_wd(nc.scalar.copy, wd_raw0, "wd16_0", 36 * KB)
-                wd16_1 = cast_wd(nc.vector.tensor_copy, wd_raw1, "wd16_1", 40 * KB)
-            piece = ready.pop(0) if ready else None
-            if piece:
+            if k in (1, 2):
+                wd16 = cast_wd(nc.vector.tensor_copy, wd_raw[:, (k - 1) * 4 * N : k * 4 * N], f"wd16_{k}", (46 + 4 * k) * KB)
+            pieces = []
+            while ready and sum(j1 - j0 for i, j0, j1 in pieces) < units[k][1] - units[k][0]:
+                pieces.append(ready.pop(0))
+            for piece in pieces:
                 back(*piece)
             vote(k)
-            if piece:
+            for piece in pieces:
                 place(*piece)
-            if k > 0 and units[k - 1][1] == 1:
-                j = units[k - 1][0]
-                ready += [(i, j * UN, (j + 1) * UN) for i in range(2)]
-            if k == 0:
-                quantise([x[:] for x in wa_qs[1]], wa16_1[:])
-            if k == LEAD - 1:
-                quantise([x[:] for x in wd_qs[0]], wd16_0[:])
-                quantise([x[:] for x in wd_qs[1]], wd16_1[:])
-                clear_page(2, 36 * KB)
+            if k > 0 and units[k - 1][2] == 1:
+                j0, j1 = units[k - 1][:2]
+                ready += [(i, j0, j1) for i in range(3 if j1 <= SPLIT2 else 2)]
+            if k in (1, 2):
+                quantise([x[:] for x in wd_qs[k - 1]], wd16[:])
+            if k == CLEAR3:
+                clear_page(3, 58 * KB)
 
-        clear_page(3, 0)
-        for piece in ready:
+        fill = ready + [(3, 0, PASS)]
+        for piece in fill:
             back(*piece)
-        place(*ready.pop(0))
-        nc.vector.tensor_tensor(slot(last + 1, HH), slot(last + 1, LO), slot(last + 1, MID), ALU.max)
-        place(*ready.pop(0))
+        place(*fill[0])
+        nc.vector.tensor_tensor(slot(last + 1, "h"), slot(last + 1, "lo"), slot(last + 1, "mid"), ALU.max)
+        place(*fill[1])
         quantise_h(last)
-        for piece in ready:
-            place(*piece)
-        back(2, 0, PASS)
-        place(2, 0, PASS)
+        place(*fill[2])
         for i in range(2):
             back(i, S - UN, S)
             place(i, S - UN, S)
             nc.sync.dma_start(out_v[:, i, :], pages[i][:])
-        back(2, PASS, S)
-        place(2, PASS, S)
+        back(2, SPLIT2, S - UN)
+        back(2, S - UN, S)
+        place(2, SPLIT2, S)
         nc.sync.dma_start(out_v[:, 2, :], pages[2][:])
-        back(3, 0, PASS)
         back(3, PASS, S)
-        place(3, 0, S)
+        place(3, PASS, S)
         nc.sync.dma_start(out_v[:, 3, :], pages[3][:])

@@ -24,7 +24,6 @@ WIDE = 2 * UN
 FIRST = 256
 LEAD = 3
 REGIONS = 7
-CLEAR3 = 8
 SPLIT2 = 640
 KB = 1024
 
@@ -62,13 +61,13 @@ def tile_list_median_codeword_repair_kernel(
         wb_raw = kept([P, H // 2], I32, "wb_raw", "raw_b")
         wc_raw = kept([P, H], I32, "wc_raw", "raw_c")
         nc.scalar.dma_start(wa_raw0[:].rearrange("p (j c) -> p j c", j=4), wa_v[:, :, 0:PASS])
-        wa_raw1 = placed([P, 4 * PASS], F32, "wa_raw1", 72 * KB)
+        wa_raw1 = placed([P, 4 * PASS], F32, "wa_raw1", 58 * KB)
         nc.scalar.dma_start(wa_raw1[:].rearrange("p (j c) -> p j c", j=4), wa_v[:, :, PASS:])
         nc.scalar.dma_start(tab[:].bitcast(I32), tab_words[0].rearrange("p n t -> p (n t)").bitcast(I32))
         nc.scalar.dma_start(wb_raw[:], wb_words[0].bitcast(I32))
         nc.scalar.dma_start(wc_raw[:], wc_words[0].rearrange("p n t -> p (n t)").bitcast(I32))
 
-        pages = [kept([P, T2], F32, f"page{i}") for i in range(3)]
+        pages = [kept([P, T2], F32, f"page{i}") for i in range(4)]
 
         g_sc = placed([P, S], U8, "g_sc", 15 * KB // 2)
         nc.vector.tensor_copy(g_sc[:], tab_sc[:].indirect(idx[:]))
@@ -102,7 +101,7 @@ def tile_list_median_codeword_repair_kernel(
 
         def cast_wd(copy, raw, name, offset):
             w16 = placed([P, 4 * N], BF16, name, offset)
-            copy(w16[:].rearrange("p (i m t) -> p m i t", i=4, t=4), raw.rearrange("p (t m i) -> p m i t", t=4, i=4))
+            copy(w16[:].rearrange("p (i c v t) -> p i c v t", i=4, v=4, t=4), raw.rearrange("p (t c i v) -> p i c v t", t=4, i=4, v=4))
             return w16
 
         def quantise(qs, w16):
@@ -133,13 +132,15 @@ def tile_list_median_codeword_repair_kernel(
         nc.vector.tensor_copy(g_w[:, FIRST:], tab[:].indirect(idx[:, FIRST // 16 :]))
 
 
-        wgo_sb = placed([P, S], F32, "wgo_sb", 72 * KB)
+        wgo_sb = placed([P, S], F32, "wgo_sb", 58 * KB)
         nc.sync.dma_start(wgo_sb[:], wgo)
-        affine = placed([P, 16], F32, "affine", 76 * KB)
-        nc.sync.dma_start(affine[:, 0:4], gd.rearrange("(p i) -> p i", i=4))
-        nc.sync.dma_start(affine[:, 8:12], bd.rearrange("(p i) -> p i", i=4))
+        affine = placed([P, 16], F32, "affine", 62 * KB)
+        with nc.allow_non_contiguous_dma(reason="one gain and one bias for each partition and page"):
+            for v in range(4):
+                nc.sync.dma_start(affine[v:P:4, 0:4], gd.rearrange("(c i v) -> v c i", i=4, v=4)[v])
+                nc.sync.dma_start(affine[v:P:4, 8:12], bd.rearrange("(c i v) -> v c i", i=4, v=4)[v])
 
-        for i in range(3):
+        for i in range(4):
             for q in range(2):
                 nc.vector.memset(pages[i][:, q * T2 // 2 : (q + 1) * T2 // 2].bitcast(I32), 0)
 
@@ -152,7 +153,7 @@ def tile_list_median_codeword_repair_kernel(
         last = len(units) - 1
 
         size = 7 * 4 * WIDE
-        regions = [kept([P, size], BF16, "region0"), placed([P, size], BF16, "region1", 58 * KB), kept([P, size], BF16, "region2")]
+        regions = [kept([P, size], BF16, f"region{e}") for e in range(LEAD)]
         regions += [placed([P, size], BF16, f"region{LEAD}", 20 * KB), placed([P, size], BF16, f"region{LEAD + 1}", 34 * KB)]
         regions += [kept([P, size], BF16, f"region{e}") for e in range(LEAD + 2, REGIONS)]
         y = [kept([P, S], F32, f"y{i}") for i in range(4)]
@@ -222,12 +223,7 @@ def tile_list_median_codeword_repair_kernel(
         def place(i, j0, j1):
             nc.vector.tensor_tensor(pages[i][:].indirect(idx2[:, j0 // 16 : j1 // 16]), y[i][:, j0:j1], wgo_sb[:, j0:j1], ALU.mult)
 
-        def clear_page(i, offset):
-            pages.append(placed([P, T2], F32, f"page{i}", offset))
-            for q in range(4):
-                nc.gpsimd.memset(pages[i][:, q * T2 // 4 : (q + 1) * T2 // 4].bitcast(I32), 0)
-
-        out_v = out.rearrange("(p i) t -> p i t", i=4)
+        out_v = out.rearrange("(c i v) t -> i c v t", i=4, v=4)
         ready = []
         for k in range(len(units)):
             estimates(k)
@@ -246,10 +242,8 @@ def tile_list_median_codeword_repair_kernel(
                 ready += [(i, j0, j1) for i in range(3 if j1 <= SPLIT2 else 2)]
             if k in (1, 2):
                 quantise([x[:] for x in wd_qs[k - 1]], wd16[:])
-            if k == CLEAR3:
-                clear_page(3, 58 * KB)
 
-        fill = ready + [(3, 0, PASS)]
+        fill = ready + [(3, 0, WIDE)]
         for piece in fill:
             back(*piece)
         place(*fill[0])
@@ -260,11 +254,12 @@ def tile_list_median_codeword_repair_kernel(
         for i in range(2):
             back(i, S - UN, S)
             place(i, S - UN, S)
-            nc.sync.dma_start(out_v[:, i, :], pages[i][:])
+            nc.sync.dma_start(out_v[i], pages[i][:])
         back(2, SPLIT2, S - UN)
         back(2, S - UN, S)
         place(2, SPLIT2, S)
-        nc.sync.dma_start(out_v[:, 2, :], pages[2][:])
+        nc.sync.dma_start(out_v[2], pages[2][:])
+        back(3, WIDE, PASS)
         back(3, PASS, S)
-        place(3, PASS, S)
-        nc.sync.dma_start(out_v[:, 3, :], pages[3][:])
+        place(3, WIDE, S)
+        nc.sync.dma_start(out_v[3], pages[3][:])

@@ -21,10 +21,8 @@ PASS = 512
 HB = H // PASS
 UN = 128
 WIDE = 2 * UN
-FIRST = 256
-LEAD = 3
-REGIONS = 7
-SPLIT2 = 640
+HALF = S // 2
+REGIONS = 6
 KB = 1024
 
 
@@ -47,28 +45,56 @@ def tile_list_median_codeword_repair_kernel(
         idx2 = kept([P, S // 16], U16, "idx2")
         nc.sync.dma_start(idx[:], offs)
 
-        tab_sc = placed([P, T], U8, "tab_sc", 3 * KB)
-        w_sc = kept([P, 2 * H], U8, "w_sc")
+        tab_sc = placed([P, T], U8, "tab_sc", 1 * KB)
+        w_sc = placed([P, 2 * H], U8, "w_sc", 13 * KB)
         nc.scalar.dma_start(tab_sc[:].bitcast(I32), tab_scales[0].bitcast(I32).unsqueeze(1).to_broadcast([16, 8, T // 4]))
-        nc.sync.dma_start(w_sc[:, 0:H].bitcast(I32), wb_scales[0].bitcast(I32).unsqueeze(1).to_broadcast([16, 8, H // 4]))
+        nc.scalar.dma_start(w_sc[:, 0:H].bitcast(I32), wb_scales[0].bitcast(I32).unsqueeze(1).to_broadcast([16, 8, H // 4]))
         nc.scalar.dma_start(w_sc[:, H : 2 * H].bitcast(I32), wc_scales[0].bitcast(I32).unsqueeze(1).to_broadcast([16, 8, H // 4]))
-
         nc.sync.dma_start(idx2[:], offs2)
 
-        wa_v = wa.rearrange("(p j) c -> p j c", j=4)
-        wa_raw0 = placed([P, 4 * PASS], F32, "wa_raw0", 16 * KB)
+        warm = kept([P, 16], F32, "warm")
+        nc.gpsimd.memset(warm[:, 0:1], 0.0)
+        nc.scalar.activation(warm[:, 8:9], warm[:, 0:1], IDENT)
+
+        def load_wa(b, raw):
+            nc.sync.dma_start(raw[:].rearrange("p (j c) -> p j c", j=4), wa.rearrange("(p j) c -> p j c", j=4)[:, :, b * PASS : (b + 1) * PASS])
+            return raw
+
+        def load_wd(b, raw):
+            rows = wd[b * PASS : (b + 1) * PASS, :].rearrange("(c t v) n -> t c (v n)", t=4, v=4)
+            for t in range(4):
+                nc.sync.dma_start(raw[:, t * N : (t + 1) * N], rows[t])
+            return raw
+
         tab = kept([P, T], U32, "tab")
-        wb_raw = kept([P, H // 2], I32, "wb_raw", "raw_b")
-        wc_raw = kept([P, H], I32, "wc_raw", "raw_c")
-        nc.scalar.dma_start(wa_raw0[:].rearrange("p (j c) -> p j c", j=4), wa_v[:, :, 0:PASS])
-        wa_raw1 = placed([P, 4 * PASS], F32, "wa_raw1", 58 * KB)
-        nc.scalar.dma_start(wa_raw1[:].rearrange("p (j c) -> p j c", j=4), wa_v[:, :, PASS:])
-        nc.scalar.dma_start(tab[:].bitcast(I32), tab_words[0].rearrange("p n t -> p (n t)").bitcast(I32))
-        nc.scalar.dma_start(wb_raw[:], wb_words[0].bitcast(I32))
-        nc.scalar.dma_start(wc_raw[:], wc_words[0].rearrange("p n t -> p (n t)").bitcast(I32))
+        nc.sync.dma_start(tab[:].bitcast(I32), tab_words[0].rearrange("p n t -> p (n t)").bitcast(I32))
+        wa_raw0 = load_wa(0, placed([P, 4 * PASS], F32, "wa_raw0", 16 * KB))
+        wb_raw = placed([P, H // 2], I32, "wb_raw", 43 * KB)
+        wc_raw = placed([P, H], I32, "wc_raw", 56 * KB)
+        nc.sync.dma_start(wb_raw[:], wb_words[0].bitcast(I32))
+        nc.sync.dma_start(wc_raw[:], wc_words[0].rearrange("p n t -> p (n t)").bitcast(I32))
+
+        def quantised(name, width):
+            return kept([P, width], U32, name + "_q"), kept([P, width], U8, name + "_s")
+
+        def cast_wa(copy, raw, w16):
+            copy(w16[:].rearrange("p (t c v j) -> p t c v j", t=4, v=4, j=4), raw[:].rearrange("p (j c t v) -> p t c v j", j=4, t=4, v=4))
+            return w16
+
+        def cast_wd(copy, raw, w16):
+            copy(w16[:].rearrange("p (i c v t) -> p i c v t", i=4, v=4, t=4), raw[:].rearrange("p (t c i v) -> p i c v t", t=4, i=4, v=4))
+            return w16
+
+        def quantise(qs, w16):
+            nc.vector.quantize_mx(qs[0].bitcast(FP8X4), qs[1], w16)
 
         pages = [kept([P, T2], F32, f"page{i}") for i in range(4)]
 
+        def clear(i, half):
+            nc.vector.memset(pages[i][:, half * T2 // 2 : (half + 1) * T2 // 2].bitcast(I32), 0)
+
+        for i in range(2):
+            nc.vector.memset(pages[i][:].bitcast(I32), 0)
         g_sc = placed([P, S], U8, "g_sc", 15 * KB // 2)
         nc.vector.tensor_copy(g_sc[:], tab_sc[:].indirect(idx[:]))
         planes = kept([P, S + 2 * H], U8, "planes")
@@ -78,87 +104,59 @@ def tile_list_median_codeword_repair_kernel(
             w_sc[:].bitcast(I32).rearrange("p (a c t) -> p a t c", t=4, c=32),
         )
         for r in range(1, 4):
-            nc.sync.dma_start(planes[r:P:32, :].bitcast(I32), planes[8 * r : P : 32, :].bitcast(I32))
+            nc.scalar.dma_start(planes[r:P:32, :].bitcast(I32), planes[8 * r : P : 32, :].bitcast(I32))
 
-        wd_raw = placed([P, HB * 4 * N], F32, "wd_raw", 20 * KB)
-        wd_raw0, wd_raw1 = wd_raw[:, 0 : 4 * N], wd_raw[:, 4 * N :]
-
-        def load_wd(b, raw):
-            rows = wd[b * PASS : (b + 1) * PASS, :].rearrange("(c t v) n -> t c (v n)", t=4, v=4)
-            for t in range(4):
-                nc.sync.dma_start(raw[:, t * N : (t + 1) * N], rows[t])
-
-        load_wd(0, wd_raw0)
-        load_wd(1, wd_raw1)
-
-        def quantised(name, width):
-            return kept([P, width], U32, name + "_q"), kept([P, width], U8, name + "_s")
-
-        def cast_wa(copy, raw, name):
-            w16 = kept([P, 4 * PASS], BF16, name)
-            copy(w16[:].rearrange("p (t c v j) -> p t c v j", t=4, v=4, j=4), raw[:].rearrange("p (j c t v) -> p t c v j", j=4, t=4, v=4))
-            return w16
-
-        def cast_wd(copy, raw, name, offset):
-            w16 = placed([P, 4 * N], BF16, name, offset)
-            copy(w16[:].rearrange("p (i c v t) -> p i c v t", i=4, v=4, t=4), raw.rearrange("p (t c i v) -> p i c v t", t=4, i=4, v=4))
-            return w16
-
-        def quantise(qs, w16):
-            nc.vector.quantize_mx(qs[0].bitcast(FP8X4), qs[1], w16)
-
-        wa_qs = [(placed([P, PASS], U32, "wa0_q", 4 * KB), kept([P, PASS], U8, "wa0_s")), quantised("wa1", PASS)]
+        wa_qs = [(placed([P, PASS], U32, f"wa{b}_q", (12 + 2 * b) * KB), kept([P, PASS], U8, f"wa{b}_s")) for b in range(HB)]
         wd_qs = [quantised(f"wd{b}", N) for b in range(HB)]
         h_qs = [quantised(f"h{b}", S) for b in range(HB)]
 
-        wa16_0 = cast_wa(nc.scalar.copy, wa_raw0, "wa16_0")
-        wa16_1 = cast_wa(nc.scalar.copy, wa_raw1, "wa16_1")
-
-
-        g_w = placed([P, S], U32, "g_w", 0)
-        nc.vector.tensor_copy(g_w[:, 0:FIRST], tab[:].indirect(idx[:, 0 : FIRST // 16]))
+        wa16_0 = cast_wa(nc.scalar.copy, wa_raw0, kept([P, 4 * PASS], BF16, "wa16_0"))
+        g_w = [placed([P, HALF], U32, "g_lo", 0)]
+        nc.vector.tensor_copy(g_w[0][:], tab[:].indirect(idx[:, 0 : HALF // 16]))
+        clear(2, 0)
         wb_q = placed([P, H // 2], I32, "wb_q", 6 * KB)
         wc_q = placed([P, H], I32, "wc_q", 8 * KB)
         nc.vector.tensor_copy(
             wb_q[:].rearrange("p (b t c v) -> p b t c v", b=HB, t=4, v=2),
             wb_raw[:].rearrange("p (b c t v) -> p b t c v", b=HB, t=4, v=2),
         )
+        clear(2, 1)
+        clear(3, 0)
         nc.vector.tensor_copy(
             wc_q[:].rearrange("p (b t c v) -> p b t c v", b=HB, t=4, v=4),
             wc_raw[:].rearrange("p (b c t v) -> p b t c v", b=HB, t=4, v=4),
         )
+        clear(3, 1)
         quantise([x[:] for x in wa_qs[0]], wa16_0[:])
-        quantise([x[:] for x in wa_qs[1]], wa16_1[:])
-        nc.vector.tensor_copy(g_w[:, FIRST:], tab[:].indirect(idx[:, FIRST // 16 :]))
+        wa_raw1 = load_wa(1, placed([P, 4 * PASS], F32, "wa_raw1", 36 * KB))
+        wa16_1 = cast_wa(nc.vector.tensor_copy, wa_raw1, kept([P, 4 * PASS], BF16, "wa16_1"))
 
-
-        wgo_sb = placed([P, S], F32, "wgo_sb", 58 * KB)
+        wd_raw0 = load_wd(0, placed([P, 4 * N], F32, "wd_raw0", 44 * KB))
+        wd_raw1 = load_wd(1, placed([P, 4 * N], F32, "wd_raw1", 52 * KB))
+        wgo_sb = placed([P, S], F32, "wgo_sb", 16 * KB)
         nc.sync.dma_start(wgo_sb[:], wgo)
-        affine = placed([P, 16], F32, "affine", 62 * KB)
+        affine = kept([P, 16], F32, "affine")
         with nc.allow_non_contiguous_dma(reason="one gain and one bias for each partition and page"):
             for v in range(4):
-                nc.sync.dma_start(affine[v:P:4, 0:4], gd.rearrange("(c i v) -> v c i", i=4, v=4)[v])
-                nc.sync.dma_start(affine[v:P:4, 8:12], bd.rearrange("(c i v) -> v c i", i=4, v=4)[v])
-
-        for i in range(4):
-            for q in range(2):
-                nc.vector.memset(pages[i][:, q * T2 // 2 : (q + 1) * T2 // 2].bitcast(I32), 0)
+                nc.gpsimd.dma_start(affine[v:P:4, 0:4], gd.rearrange("(c i v) -> v c i", i=4, v=4)[v])
+                nc.gpsimd.dma_start(affine[v:P:4, 8:12], bd.rearrange("(c i v) -> v c i", i=4, v=4)[v])
 
         est_banks = [psum.tile([P, 4, UN], F32, name=f"est_bank{e}") for e in range(6)]
         y_banks = [psum.tile([P, PASS], F32, name=f"y_bank{e}") for e in range(2)]
-        spans = [(j * UN, (j + 1) * UN) for j in range(LEAD)]
-        units = [(j0, j1, b) for j0, j1 in spans for b in range(HB)]
-        spans = [(j0, j0 + WIDE) for j0 in range(LEAD * UN, S - UN, WIDE)] + [(S - UN, S)]
-        units += [(j0, j1, b) for j0, j1 in spans for b in range(HB)]
+        units = [(j0, j0 + UN, b) for b in range(HB) for j0 in (0, UN)]
+        units += [(j0, j0 + WIDE, b) for j0 in range(WIDE, S, WIDE) for b in range(HB)]
         last = len(units) - 1
 
         size = 7 * 4 * WIDE
-        regions = [kept([P, size], BF16, f"region{e}") for e in range(LEAD)]
-        regions += [placed([P, size], BF16, f"region{LEAD}", 20 * KB), placed([P, size], BF16, f"region{LEAD + 1}", 34 * KB)]
-        regions += [kept([P, size], BF16, f"region{e}") for e in range(LEAD + 2, REGIONS)]
+        regions = [kept([P, size], BF16, f"region{e}") for e in range(3)]
+        regions += [placed([P, size], BF16, "region3", 34 * KB), placed([P, size], BF16, "region4", 48 * KB)]
+        regions += [kept([P, size], BF16, f"region{e}") for e in range(5, REGIONS)]
+        apart = kept([P, 3, 4 * UN], BF16, "apart")
         y = [kept([P, S], F32, f"y{i}") for i in range(4)]
 
         def slot(k, first, end=None):
+            if k == 3 and first in ("lo", "mid", "h"):
+                return apart[:, ("lo", "mid", "h").index(first), :]
             before = 4 * (units[k - 1][1] - units[k - 1][0]) if k > 0 else 0
             own = 4 * (units[k][1] - units[k][0]) if k <= last else 0
             widths = [before, own, before, own, before, own, own]
@@ -170,9 +168,9 @@ def tile_list_median_codeword_repair_kernel(
 
         def estimates(k):
             j0, j1, b = units[k]
-            order = ("x1", "x2", "x0") if k == 0 else ("x0", "x1", "x2")
+            order = ("x1", "x2", "x0") if k in (0, 2) else ("x0", "x1", "x2")
             for j in range(j0, j1, UN):
-                rhs = g_w[:, j : j + UN].bitcast(FP8X4)
+                rhs = g_w[j // HALF][:, j % HALF : j % HALF + UN].bitcast(FP8X4)
                 rhs_s = planes[:, j : j + UN]
                 for x in order:
                     bank = est_banks[len(filled) % len(est_banks)]
@@ -197,10 +195,13 @@ def tile_list_median_codeword_repair_kernel(
             quantise([x[:, j0:j1] for x in h_qs[b]], slot(k + 1, "h"))
 
         def vote(k):
-            nc.vector.tensor_tensor(slot(k, "h", "hi"), slot(k, "lo", "x1"), slot(k, "mid", "x2"), ALU.max)
+            if k == 3:
+                nc.vector.tensor_tensor(slot(k, "hi"), slot(k, "x1"), slot(k, "x2"), ALU.max)
+            else:
+                nc.vector.tensor_tensor(slot(k, "h", "hi"), slot(k, "lo", "x1"), slot(k, "mid", "x2"), ALU.max)
             nc.vector.tensor_tensor(slot(k + 1, "lo"), slot(k, "x1"), slot(k, "x2"), ALU.min)
             nc.vector.tensor_tensor(slot(k + 1, "mid"), slot(k, "hi"), slot(k, "x0"), ALU.min)
-            if k > 0:
+            if k not in (0, 3):
                 quantise_h(k - 1)
 
         made = []
@@ -227,8 +228,6 @@ def tile_list_median_codeword_repair_kernel(
         ready = []
         for k in range(len(units)):
             estimates(k)
-            if k in (1, 2):
-                wd16 = cast_wd(nc.vector.tensor_copy, wd_raw[:, (k - 1) * 4 * N : k * 4 * N], f"wd16_{k}", (46 + 4 * k) * KB)
             pieces = []
             while ready and sum(j1 - j0 for i, j0, j1 in pieces) < units[k][1] - units[k][0]:
                 pieces.append(ready.pop(0))
@@ -237,11 +236,21 @@ def tile_list_median_codeword_repair_kernel(
             vote(k)
             for piece in pieces:
                 place(*piece)
-            if k > 0 and units[k - 1][2] == 1:
-                j0, j1 = units[k - 1][:2]
-                ready += [(i, j0, j1) for i in range(3 if j1 <= SPLIT2 else 2)]
-            if k in (1, 2):
-                quantise([x[:] for x in wd_qs[k - 1]], wd16[:])
+            if k == 0:
+                quantise([x[:] for x in wa_qs[1]], wa16_1[:])
+            if k == 2:
+                wd16_0 = cast_wd(nc.scalar.copy, wd_raw0, kept([P, 4 * N], BF16, "wd16_0"))
+                nc.vector.tensor_tensor(slot(k + 1, "h"), slot(k + 1, "lo"), slot(k + 1, "mid"), ALU.max)
+                wd16_1 = cast_wd(nc.vector.tensor_copy, wd_raw1, placed([P, 4 * N], BF16, "wd16_1", 62 * KB))
+                quantise_h(k)
+                quantise([x[:] for x in wd_qs[0]], wd16_0[:])
+                quantise([x[:] for x in wd_qs[1]], wd16_1[:])
+            if k == 3:
+                g_w.append(placed([P, HALF], U32, "g_hi", 62 * KB))
+                nc.vector.tensor_copy(g_w[1][:], tab[:].indirect(idx[:, HALF // 16 :]))
+            if k == 2 or k > 3 and units[k - 1][2] == 1:
+                j0, j1 = units[max(k - 1, 2)][:2]
+                ready += [(i, j0, j1) for i in range(3 if j1 <= HALF else 2)]
 
         fill = ready + [(3, 0, WIDE)]
         for piece in fill:
@@ -250,16 +259,16 @@ def tile_list_median_codeword_repair_kernel(
         nc.vector.tensor_tensor(slot(last + 1, "h"), slot(last + 1, "lo"), slot(last + 1, "mid"), ALU.max)
         place(*fill[1])
         quantise_h(last)
-        place(*fill[2])
+        for piece in fill[2:]:
+            place(*piece)
         for i in range(2):
-            back(i, S - UN, S)
-            place(i, S - UN, S)
+            back(i, S - WIDE, S)
+            place(i, S - WIDE, S)
             nc.sync.dma_start(out_v[i], pages[i][:])
-        back(2, SPLIT2, S - UN)
-        back(2, S - UN, S)
-        place(2, SPLIT2, S)
+        back(2, HALF, S)
+        place(2, HALF, S)
         nc.sync.dma_start(out_v[2], pages[2][:])
-        back(3, WIDE, PASS)
-        back(3, PASS, S)
+        back(3, WIDE, HALF)
+        back(3, HALF, S)
         place(3, WIDE, S)
         nc.sync.dma_start(out_v[3], pages[3][:])

@@ -78,11 +78,11 @@ def tile_list_median_codeword_repair_kernel(
             return kept([P, width], U32, name + "_q"), kept([P, width], U8, name + "_s")
 
         def cast_wa(copy, raw, w16):
-            copy(w16[:].rearrange("p (t c v j) -> p t c v j", t=4, v=4, j=4), raw[:].rearrange("p (j c t v) -> p t c v j", j=4, t=4, v=4))
+            copy(w16[:].rearrange("p (t c v j) -> p t c j v", t=4, v=4, j=4), raw[:].rearrange("p (j c t v) -> p t c j v", j=4, t=4, v=4))
             return w16
 
         def cast_wd(copy, raw, w16):
-            copy(w16[:].rearrange("p (i c v t) -> p i c v t", i=4, v=4, t=4), raw[:].rearrange("p (t c i v) -> p i c v t", t=4, i=4, v=4))
+            copy(w16[:].rearrange("p (i c v t) -> p i c t v", i=4, v=4, t=4), raw[:].rearrange("p (t c i v) -> p i c t v", t=4, i=4, v=4))
             return w16
 
         def quantise(qs, w16):

@@ -99,9 +99,9 @@ def tile_list_median_codeword_repair_kernel(
         nc.vector.tensor_copy(g_sc[:], tab_sc[:].indirect(idx[:]))
         planes = kept([P, S + 2 * H], U8, "planes")
         nc.vector.tensor_copy(planes[:, 0:S].bitcast(I32), g_sc[:].bitcast(I32))
-        nc.vector.tensor_copy(
-            planes[:, S:].bitcast(I32).rearrange("p (a t c) -> p a t c", t=4, c=32),
-            w_sc[:].bitcast(I32).rearrange("p (a c t) -> p a t c", t=4, c=32),
+        nc.scalar.copy(
+            planes[:, S:].bitcast(U32).rearrange("p (a t c) -> p a t c", t=4, c=32),
+            w_sc[:].bitcast(U32).rearrange("p (a c t) -> p a t c", t=4, c=32),
         )
         for r in range(1, 4):
             nc.scalar.dma_start(planes[r:P:32, :].bitcast(I32), planes[8 * r : P : 32, :].bitcast(I32))
@@ -129,12 +129,10 @@ def tile_list_median_codeword_repair_kernel(
         clear(3, 1)
         quantise([x[:] for x in wa_qs[0]], wa16_0[:])
         wa_raw1 = load_wa(1, placed([P, 4 * PASS], F32, "wa_raw1", 36 * KB))
-        wa16_1 = cast_wa(nc.vector.tensor_copy, wa_raw1, kept([P, 4 * PASS], BF16, "wa16_1"))
+        wa16_1 = cast_wa(nc.vector.tensor_copy, wa_raw1, placed([P, 4 * PASS], BF16, "wa16_1", 66 * KB))
 
         wd_raw0 = load_wd(0, placed([P, 4 * N], F32, "wd_raw0", 44 * KB))
         wd_raw1 = load_wd(1, placed([P, 4 * N], F32, "wd_raw1", 52 * KB))
-        wgo_sb = placed([P, S], F32, "wgo_sb", 16 * KB)
-        nc.sync.dma_start(wgo_sb[:], wgo)
         affine = kept([P, 16], F32, "affine")
         with nc.allow_non_contiguous_dma(reason="one gain and one bias for each partition and page"):
             for v in range(4):
@@ -238,6 +236,8 @@ def tile_list_median_codeword_repair_kernel(
                 place(*piece)
             if k == 0:
                 quantise([x[:] for x in wa_qs[1]], wa16_1[:])
+                wgo_sb = placed([P, S], F32, "wgo_sb", 66 * KB)
+                nc.sync.dma_start(wgo_sb[:], wgo)
             if k == 2:
                 wd16_0 = cast_wd(nc.scalar.copy, wd_raw0, kept([P, 4 * N], BF16, "wd16_0"))
                 nc.vector.tensor_tensor(slot(k + 1, "h"), slot(k + 1, "lo"), slot(k + 1, "mid"), ALU.max)

@@ -46,14 +46,16 @@ def tile_list_median_codeword_repair_kernel(
         nc.sync.dma_start(idx[:], offs)
 
         tab_sc = placed([P, T], U8, "tab_sc", 1 * KB)
-        w_sc = placed([P, 2 * H], U8, "w_sc", 13 * KB)
+        w_sc = placed([16, 2 * H], U8, "w_sc", 13 * KB)
         nc.scalar.dma_start(tab_sc[:].bitcast(I32), tab_scales[0].bitcast(I32).unsqueeze(1).to_broadcast([16, 8, T // 4]))
-        nc.scalar.dma_start(w_sc[:, 0:H].bitcast(I32), wb_scales[0].bitcast(I32).unsqueeze(1).to_broadcast([16, 8, H // 4]))
-        nc.scalar.dma_start(w_sc[:, H : 2 * H].bitcast(I32), wc_scales[0].bitcast(I32).unsqueeze(1).to_broadcast([16, 8, H // 4]))
+        nc.scalar.dma_start(w_sc[:, 0:H].bitcast(I32), wb_scales[0].bitcast(I32))
+        nc.scalar.dma_start(w_sc[:, H : 2 * H].bitcast(I32), wc_scales[0].bitcast(I32))
         nc.sync.dma_start(idx2[:], offs2)
 
         warm = kept([P, 16], F32, "warm")
         nc.gpsimd.memset(warm[:, 0:1], 0.0)
+        w_planes = kept([P, 2 * H], U8, "w_planes")
+        nc.gpsimd.memset(w_planes[:].bitcast(I32), 0)
         nc.scalar.activation(warm[:, 8:9], warm[:, 0:1], IDENT)
 
         def load_wa(b, raw):
@@ -77,8 +79,8 @@ def tile_list_median_codeword_repair_kernel(
         def quantised(name, width):
             return kept([P, width], U32, name + "_q"), kept([P, width], U8, name + "_s")
 
-        def cast_wa(copy, raw, w16):
-            copy(w16[:].rearrange("p (t c v j) -> p t c j v", t=4, v=4, j=4), raw[:].rearrange("p (j c t v) -> p t c j v", j=4, t=4, v=4))
+        def cast_wa(copy, raw, w16, t0=0, t1=4):
+            copy(w16[:].rearrange("p (t c v j) -> p t c j v", t=4, v=4, j=4)[:, t0:t1], raw[:].rearrange("p (j c t v) -> p t c j v", j=4, t=4, v=4)[:, t0:t1])
             return w16
 
         def cast_wd(copy, raw, w16):
@@ -88,7 +90,8 @@ def tile_list_median_codeword_repair_kernel(
         def quantise(qs, w16):
             nc.vector.quantize_mx(qs[0].bitcast(FP8X4), qs[1], w16)
 
-        pages = [kept([P, T2], F32, f"page{i}") for i in range(4)]
+        pages = [kept([P, T2], F32, f"page{i}") for i in range(3)]
+        pages.append(placed([P, T2], F32, "page3", 70 * KB))
 
         def clear(i, half):
             nc.vector.memset(pages[i][:, half * T2 // 2 : (half + 1) * T2 // 2].bitcast(I32), 0)
@@ -97,12 +100,14 @@ def tile_list_median_codeword_repair_kernel(
             nc.vector.memset(pages[i][:].bitcast(I32), 0)
         g_sc = placed([P, S], U8, "g_sc", 15 * KB // 2)
         nc.vector.tensor_copy(g_sc[:], tab_sc[:].indirect(idx[:]))
-        planes = kept([P, S + 2 * H], U8, "planes")
-        nc.vector.tensor_copy(planes[:, 0:S].bitcast(I32), g_sc[:].bitcast(I32))
         nc.scalar.copy(
-            planes[:, S:].bitcast(U32).rearrange("p (a t c) -> p a t c", t=4, c=32),
+            w_planes[0:16, :].bitcast(U32).rearrange("p (a t c) -> p a t c", t=4, c=32),
             w_sc[:].bitcast(U32).rearrange("p (a c t) -> p a t c", t=4, c=32),
         )
+        for d in range(1, 4):
+            nc.scalar.dma_start(w_planes[32 * d : 32 * d + 4, :].bitcast(I32), w_planes[4 * d : 4 * d + 4, :].bitcast(I32))
+        planes = kept([P, S], U8, "planes")
+        nc.vector.tensor_copy(planes[:].bitcast(I32), g_sc[:].bitcast(I32))
         for r in range(1, 4):
             nc.scalar.dma_start(planes[r:P:32, :].bitcast(I32), planes[8 * r : P : 32, :].bitcast(I32))
 
@@ -110,10 +115,11 @@ def tile_list_median_codeword_repair_kernel(
         wd_qs = [quantised(f"wd{b}", N) for b in range(HB)]
         h_qs = [quantised(f"h{b}", S) for b in range(HB)]
 
-        wa16_0 = cast_wa(nc.scalar.copy, wa_raw0, kept([P, 4 * PASS], BF16, "wa16_0"))
+        wa16_0 = cast_wa(nc.scalar.copy, wa_raw0, placed([P, 4 * PASS], BF16, "wa16_0", 76 * KB), 0, 2)
         g_w = [placed([P, HALF], U32, "g_lo", 0)]
         nc.vector.tensor_copy(g_w[0][:], tab[:].indirect(idx[:, 0 : HALF // 16]))
         clear(2, 0)
+        cast_wa(nc.vector.tensor_copy, wa_raw0, wa16_0, 2, 4)
         wb_q = placed([P, H // 2], I32, "wb_q", 6 * KB)
         wc_q = placed([P, H], I32, "wc_q", 8 * KB)
         nc.vector.tensor_copy(
@@ -121,13 +127,13 @@ def tile_list_median_codeword_repair_kernel(
             wb_raw[:].rearrange("p (b c t v) -> p b t c v", b=HB, t=4, v=2),
         )
         clear(2, 1)
-        clear(3, 0)
         nc.vector.tensor_copy(
             wc_q[:].rearrange("p (b t c v) -> p b t c v", b=HB, t=4, v=4),
             wc_raw[:].rearrange("p (b c t v) -> p b t c v", b=HB, t=4, v=4),
         )
-        clear(3, 1)
         quantise([x[:] for x in wa_qs[0]], wa16_0[:])
+        clear(3, 0)
+        clear(3, 1)
         wa_raw1 = load_wa(1, placed([P, 4 * PASS], F32, "wa_raw1", 36 * KB))
         wa16_1 = cast_wa(nc.vector.tensor_copy, wa_raw1, placed([P, 4 * PASS], BF16, "wa16_1", 66 * KB))
 
@@ -177,10 +183,10 @@ def tile_list_median_codeword_repair_kernel(
                         c0 = b * PASS + t * P
                         if x == "x1":
                             lhs = wb_q[:, c0 // 2 : (c0 + P) // 2].bitcast(FP4X4)
-                            lhs_s = planes[:, S + c0 : S + c0 + P]
+                            lhs_s = w_planes[:, c0 : c0 + P]
                         elif x == "x2":
                             lhs = wc_q[:, c0 : c0 + P].bitcast(FP8X4)
-                            lhs_s = planes[:, S + H + c0 : S + H + c0 + P]
+                            lhs_s = w_planes[:, H + c0 : H + c0 + P]
                         else:
                             lhs = wa_qs[b][0][:, t * P : (t + 1) * P].bitcast(FP8X4)
                             lhs_s = wa_qs[b][1][:, t * P : (t + 1) * P]

@@ -46,16 +46,15 @@ def tile_list_median_codeword_repair_kernel(
         nc.sync.dma_start(idx[:], offs)
 
         tab_sc = placed([P, T], U8, "tab_sc", 1 * KB)
-        w_sc = placed([16, 2 * H], U8, "w_sc", 13 * KB)
+        w_sc = placed([P, 2 * H], U8, "w_sc", 78 * KB)
         nc.scalar.dma_start(tab_sc[:].bitcast(I32), tab_scales[0].bitcast(I32).unsqueeze(1).to_broadcast([16, 8, T // 4]))
-        nc.scalar.dma_start(w_sc[:, 0:H].bitcast(I32), wb_scales[0].bitcast(I32))
-        nc.scalar.dma_start(w_sc[:, H : 2 * H].bitcast(I32), wc_scales[0].bitcast(I32))
+        nc.gpsimd.memset(w_sc[:].bitcast(I32), 0)
+        nc.scalar.dma_start(w_sc[0:P:8, 0:H].bitcast(I32), wb_scales[0].bitcast(I32))
+        nc.scalar.dma_start(w_sc[0:P:8, H : 2 * H].bitcast(I32), wc_scales[0].bitcast(I32))
         nc.sync.dma_start(idx2[:], offs2)
 
         warm = kept([P, 16], F32, "warm")
         nc.gpsimd.memset(warm[:, 0:1], 0.0)
-        w_planes = kept([P, 2 * H], U8, "w_planes")
-        nc.gpsimd.memset(w_planes[:].bitcast(I32), 0)
         nc.scalar.activation(warm[:, 8:9], warm[:, 0:1], IDENT)
 
         def load_wa(b, raw):
@@ -100,14 +99,12 @@ def tile_list_median_codeword_repair_kernel(
             nc.vector.memset(pages[i][:].bitcast(I32), 0)
         g_sc = placed([P, S], U8, "g_sc", 15 * KB // 2)
         nc.vector.tensor_copy(g_sc[:], tab_sc[:].indirect(idx[:]))
+        planes = kept([P, S + 2 * H], U8, "planes")
+        nc.vector.tensor_copy(planes[:, 0:S].bitcast(I32), g_sc[:].bitcast(I32))
         nc.scalar.copy(
-            w_planes[0:16, :].bitcast(U32).rearrange("p (a t c) -> p a t c", t=4, c=32),
+            planes[:, S:].bitcast(U32).rearrange("p (a t c) -> p a t c", t=4, c=32),
             w_sc[:].bitcast(U32).rearrange("p (a c t) -> p a t c", t=4, c=32),
         )
-        for d in range(1, 4):
-            nc.scalar.dma_start(w_planes[32 * d : 32 * d + 4, :].bitcast(I32), w_planes[4 * d : 4 * d + 4, :].bitcast(I32))
-        planes = kept([P, S], U8, "planes")
-        nc.vector.tensor_copy(planes[:].bitcast(I32), g_sc[:].bitcast(I32))
         for r in range(1, 4):
             nc.scalar.dma_start(planes[r:P:32, :].bitcast(I32), planes[8 * r : P : 32, :].bitcast(I32))
 
@@ -183,10 +180,10 @@ def tile_list_median_codeword_repair_kernel(
                         c0 = b * PASS + t * P
                         if x == "x1":
                             lhs = wb_q[:, c0 // 2 : (c0 + P) // 2].bitcast(FP4X4)
-                            lhs_s = w_planes[:, c0 : c0 + P]
+                            lhs_s = planes[:, S + c0 : S + c0 + P]
                         elif x == "x2":
                             lhs = wc_q[:, c0 : c0 + P].bitcast(FP8X4)
-                            lhs_s = w_planes[:, H + c0 : H + c0 + P]
+                            lhs_s = planes[:, S + H + c0 : S + H + c0 + P]
                         else:
                             lhs = wa_qs[b][0][:, t * P : (t + 1) * P].bitcast(FP8X4)
                             lhs_s = wa_qs[b][1][:, t * P : (t + 1) * P]

@@ -22,7 +22,8 @@ HB = H // PASS
 UN = 128
 WIDE = 2 * UN
 HALF = S // 2
-REGIONS = 6
+NARROW_UNITS = 4
+WIDE_PLACES = 5
 KB = 1024
 
 
@@ -35,8 +36,8 @@ def tile_list_median_codeword_repair_kernel(
         stage = ctx.enter_context(tc.tile_pool(name="stage", bufs=1))
         psum = ctx.enter_context(tc.psum_pool(name="psum", bufs=1))
 
-        def kept(shape, dtype, name, tag=None):
-            return keep.tile(shape, dtype, name=name, tag=tag or name, align_bytes=64)
+        def kept(shape, dtype, name):
+            return keep.tile(shape, dtype, name=name, tag=name, align_bytes=64)
 
         def placed(shape, dtype, name, offset):
             return stage.tile(shape, dtype, name=name, offset=offset, align_bytes=64)
@@ -45,13 +46,11 @@ def tile_list_median_codeword_repair_kernel(
         idx2 = kept([P, S // 16], U16, "idx2")
         nc.sync.dma_start(idx[:], offs)
 
-        tab_sc = placed([P, T], U8, "tab_sc", 1 * KB)
-        w_sc = placed([P, 2 * H], U8, "w_sc", 78 * KB)
+        tab_sc = kept([P, T], U8, "tab_sc")
+        w_sc = placed([P, 2 * H], U8, "w_sc", 27 * KB)
         nc.scalar.dma_start(tab_sc[:].bitcast(I32), tab_scales[0].bitcast(I32).unsqueeze(1).to_broadcast([16, 8, T // 4]))
-        nc.gpsimd.memset(w_sc[:].bitcast(I32), 0)
-        nc.scalar.dma_start(w_sc[0:P:8, 0:H].bitcast(I32), wb_scales[0].bitcast(I32))
-        nc.scalar.dma_start(w_sc[0:P:8, H : 2 * H].bitcast(I32), wc_scales[0].bitcast(I32))
-        nc.sync.dma_start(idx2[:], offs2)
+        for e, scales in enumerate((wb_scales, wc_scales)):
+            nc.scalar.dma_start(w_sc[:, e * H : (e + 1) * H].bitcast(I32), scales[0].bitcast(I32).unsqueeze(1).to_broadcast([16, 8, H // 4]))
 
         warm = kept([P, 16], F32, "warm")
         nc.gpsimd.memset(warm[:, 0:1], 0.0)
@@ -67,113 +66,110 @@ def tile_list_median_codeword_repair_kernel(
                 nc.sync.dma_start(raw[:, t * N : (t + 1) * N], rows[t])
             return raw
 
-        tab = kept([P, T], U32, "tab")
-        nc.sync.dma_start(tab[:].bitcast(I32), tab_words[0].rearrange("p n t -> p (n t)").bitcast(I32))
-        wa_raw0 = load_wa(0, placed([P, 4 * PASS], F32, "wa_raw0", 16 * KB))
-        wb_raw = placed([P, H // 2], I32, "wb_raw", 43 * KB)
-        wc_raw = placed([P, H], I32, "wc_raw", 56 * KB)
+        wa_raw0 = load_wa(0, placed([P, 4 * PASS], F32, "wa_raw0", 2 * KB))
+        wb_raw = placed([P, H // 2], I32, "wb_raw", 0)
+        wc_raw = placed([P, H], I32, "wc_raw", 16 * KB)
         nc.sync.dma_start(wb_raw[:], wb_words[0].bitcast(I32))
         nc.sync.dma_start(wc_raw[:], wc_words[0].rearrange("p n t -> p (n t)").bitcast(I32))
+        tab = kept([P, T], U32, "tab")
+        nc.sync.dma_start(tab[:].bitcast(I32), tab_words[0].rearrange("p n t -> p (n t)").bitcast(I32))
+        nc.sync.dma_start(idx2[:], offs2)
 
         def quantised(name, width):
             return kept([P, width], U32, name + "_q"), kept([P, width], U8, name + "_s")
 
-        def cast_wa(copy, raw, w16, t0=0, t1=4):
-            copy(w16[:].rearrange("p (t c v j) -> p t c j v", t=4, v=4, j=4)[:, t0:t1], raw[:].rearrange("p (j c t v) -> p t c j v", j=4, t=4, v=4)[:, t0:t1])
+        def cast_wa(copy, raw, w16):
+            copy(w16[:].rearrange("p (t c v j) -> p t c j v", t=4, v=4, j=4), raw[:].rearrange("p (j c t v) -> p t c j v", j=4, t=4, v=4))
             return w16
 
         def cast_wd(copy, raw, w16):
-            copy(w16[:].rearrange("p (i c v t) -> p i c t v", i=4, v=4, t=4), raw[:].rearrange("p (t c i v) -> p i c t v", t=4, i=4, v=4))
+            copy(w16[:].rearrange("p (i c t) -> p c t i", i=4, t=4), raw[:].rearrange("p (t c i) -> p c t i", t=4, i=4))
             return w16
 
         def quantise(qs, w16):
             nc.vector.quantize_mx(qs[0].bitcast(FP8X4), qs[1], w16)
 
-        pages = [kept([P, T2], F32, f"page{i}") for i in range(3)]
-        pages.append(placed([P, T2], F32, "page3", 70 * KB))
+        wa_qs = [quantised(f"wa{b}", PASS) for b in range(HB)]
+        wd_qs = [quantised(f"wd{b}", N) for b in range(HB)]
+        h_qs = [quantised(f"h{b}", S) for b in range(HB)]
+
+        pages = [kept([P, T2], F32, f"page{i}") for i in range(4)]
 
         def clear(i, half):
             nc.vector.memset(pages[i][:, half * T2 // 2 : (half + 1) * T2 // 2].bitcast(I32), 0)
 
         for i in range(2):
             nc.vector.memset(pages[i][:].bitcast(I32), 0)
-        g_sc = placed([P, S], U8, "g_sc", 15 * KB // 2)
+        g_sc = kept([P, S], U8, "g_sc")
         nc.vector.tensor_copy(g_sc[:], tab_sc[:].indirect(idx[:]))
+        clear(2, 0)
         planes = kept([P, S + 2 * H], U8, "planes")
         nc.vector.tensor_copy(planes[:, 0:S].bitcast(I32), g_sc[:].bitcast(I32))
         nc.scalar.copy(
-            planes[:, S:].bitcast(U32).rearrange("p (a t c) -> p a t c", t=4, c=32),
-            w_sc[:].bitcast(U32).rearrange("p (a c t) -> p a t c", t=4, c=32),
+            planes[:, S:].bitcast(U32).rearrange("p (a t c) -> p a c t", t=4, c=32),
+            w_sc[:].bitcast(U32).rearrange("p (a c t) -> p a c t", t=4, c=32),
         )
         for r in range(1, 4):
-            nc.scalar.dma_start(planes[r:P:32, :].bitcast(I32), planes[8 * r : P : 32, :].bitcast(I32))
-
-        wa_qs = [(placed([P, PASS], U32, f"wa{b}_q", (12 + 2 * b) * KB), kept([P, PASS], U8, f"wa{b}_s")) for b in range(HB)]
-        wd_qs = [quantised(f"wd{b}", N) for b in range(HB)]
-        h_qs = [quantised(f"h{b}", S) for b in range(HB)]
-
-        wa16_0 = cast_wa(nc.scalar.copy, wa_raw0, placed([P, 4 * PASS], BF16, "wa16_0", 76 * KB), 0, 2)
-        g_w = [placed([P, HALF], U32, "g_lo", 0)]
-        nc.vector.tensor_copy(g_w[0][:], tab[:].indirect(idx[:, 0 : HALF // 16]))
-        clear(2, 0)
-        cast_wa(nc.vector.tensor_copy, wa_raw0, wa16_0, 2, 4)
-        wb_q = placed([P, H // 2], I32, "wb_q", 6 * KB)
-        wc_q = placed([P, H], I32, "wc_q", 8 * KB)
+            nc.sync.dma_start(planes[r:P:32, :].bitcast(I32), planes[8 * r : P : 32, :].bitcast(I32))
+        wa16_0 = cast_wa(nc.scalar.copy, wa_raw0, placed([P, 4 * PASS], BF16, "wa16_0", 27 * KB))
+        wb_q = kept([P, H // 2], I32, "wb_q")
+        wc_q = kept([P, H], U32, "wc_q")
         nc.vector.tensor_copy(
-            wb_q[:].rearrange("p (b t c v) -> p b t c v", b=HB, t=4, v=2),
-            wb_raw[:].rearrange("p (b c t v) -> p b t c v", b=HB, t=4, v=2),
+            wb_q[:].rearrange("p (b t c v) -> p b c t v", b=HB, t=4, v=2),
+            wb_raw[:].rearrange("p (b c t v) -> p b c t v", b=HB, t=4, v=2),
         )
         clear(2, 1)
-        nc.vector.tensor_copy(
-            wc_q[:].rearrange("p (b t c v) -> p b t c v", b=HB, t=4, v=4),
-            wc_raw[:].rearrange("p (b c t v) -> p b t c v", b=HB, t=4, v=4),
+        clear(3, 0)
+        nc.scalar.copy(
+            wc_q[:].rearrange("p (b t c v) -> p b c t v", b=HB, t=4, v=4),
+            wc_raw[:].bitcast(U32).rearrange("p (b c t v) -> p b c t v", b=HB, t=4, v=4),
         )
         quantise([x[:] for x in wa_qs[0]], wa16_0[:])
-        clear(3, 0)
+        wa_raw1 = load_wa(1, placed([P, 4 * PASS], F32, "wa_raw1", 0))
+        wd_raw0 = load_wd(0, placed([P, 4 * N], F32, "wd_raw0", 29 * KB))
+        wd_raw1 = load_wd(1, placed([P, 4 * N], F32, "wd_raw1", 15 * KB))
         clear(3, 1)
-        wa_raw1 = load_wa(1, placed([P, 4 * PASS], F32, "wa_raw1", 36 * KB))
-        wa16_1 = cast_wa(nc.vector.tensor_copy, wa_raw1, placed([P, 4 * PASS], BF16, "wa16_1", 66 * KB))
-
-        wd_raw0 = load_wd(0, placed([P, 4 * N], F32, "wd_raw0", 44 * KB))
-        wd_raw1 = load_wd(1, placed([P, 4 * N], F32, "wd_raw1", 52 * KB))
-        affine = kept([P, 16], F32, "affine")
-        with nc.allow_non_contiguous_dma(reason="one gain and one bias for each partition and page"):
-            for v in range(4):
-                nc.gpsimd.dma_start(affine[v:P:4, 0:4], gd.rearrange("(c i v) -> v c i", i=4, v=4)[v])
-                nc.gpsimd.dma_start(affine[v:P:4, 8:12], bd.rearrange("(c i v) -> v c i", i=4, v=4)[v])
+        g_w = placed([P, S], U32, "g_w", 24 * KB)
+        nc.vector.tensor_copy(g_w[:, 0:WIDE], tab[:].indirect(idx[:, 0 : WIDE // 16]))
+        nc.vector.tensor_copy(g_w[:, WIDE:], tab[:].indirect(idx[:, WIDE // 16 :]))
+        wa16_1 = cast_wa(nc.vector.tensor_copy, wa_raw1, placed([P, 4 * PASS], BF16, "wa16_1", 10 * KB))
 
         est_banks = [psum.tile([P, 4, UN], F32, name=f"est_bank{e}") for e in range(6)]
         y_banks = [psum.tile([P, PASS], F32, name=f"y_bank{e}") for e in range(2)]
         units = [(j0, j0 + UN, b) for b in range(HB) for j0 in (0, UN)]
         units += [(j0, j0 + WIDE, b) for j0 in range(WIDE, S, WIDE) for b in range(HB)]
         last = len(units) - 1
-
-        size = 7 * 4 * WIDE
-        regions = [kept([P, size], BF16, f"region{e}") for e in range(3)]
-        regions += [placed([P, size], BF16, "region3", 34 * KB), placed([P, size], BF16, "region4", 48 * KB)]
-        regions += [kept([P, size], BF16, f"region{e}") for e in range(5, REGIONS)]
-        apart = kept([P, 3, 4 * UN], BF16, "apart")
         y = [kept([P, S], F32, f"y{i}") for i in range(4)]
 
-        def slot(k, first, end=None):
-            if k == 3 and first in ("lo", "mid", "h"):
-                return apart[:, ("lo", "mid", "h").index(first), :]
+        names = ["lo", "x1", "mid", "x2", "h", "hi", "x0"]
+
+        def widths(k):
             before = 4 * (units[k - 1][1] - units[k - 1][0]) if k > 0 else 0
             own = 4 * (units[k][1] - units[k][0]) if k <= last else 0
-            widths = [before, own, before, own, before, own, own]
-            names = ["lo", "x1", "mid", "x2", "h", "hi", "x0"]
+            return [before, own, before, own, before, own, own]
+
+        def region_offset(k):
+            if k < NARROW_UNITS:
+                return (38 + max(0, 7 * k - 3)) * KB
+            return (63 + 14 * ((k - NARROW_UNITS) % WIDE_PLACES)) * KB
+
+        regions = {}
+
+        def slot(k, first, end=None):
+            w = widths(k)
+            if k not in regions:
+                regions[k] = placed([P, sum(w)], BF16, f"region{k}", region_offset(k))
             a, z = names.index(first), names.index(end or first)
-            return regions[k % REGIONS][:, sum(widths[:a]) : sum(widths[: z + 1])]
+            return regions[k][:, sum(w[:a]) : sum(w[: z + 1])]
 
         filled = []
 
         def estimates(k):
             j0, j1, b = units[k]
-            order = ("x1", "x2", "x0") if k in (0, 2) else ("x0", "x1", "x2")
             for j in range(j0, j1, UN):
-                rhs = g_w[j // HALF][:, j % HALF : j % HALF + UN].bitcast(FP8X4)
+                rhs = g_w[:, j : j + UN].bitcast(FP8X4)
                 rhs_s = planes[:, j : j + UN]
-                for x in order:
+                for x in ("x1", "x2", "x0"):
                     bank = est_banks[len(filled) % len(est_banks)]
                     filled.append(x)
                     for t in range(4):
@@ -195,15 +191,18 @@ def tile_list_median_codeword_repair_kernel(
             j0, j1, b = units[k]
             quantise([x[:, j0:j1] for x in h_qs[b]], slot(k + 1, "h"))
 
-        def vote(k):
-            if k == 3:
-                nc.vector.tensor_tensor(slot(k, "hi"), slot(k, "x1"), slot(k, "x2"), ALU.max)
-            else:
+        def upper(k, merged):
+            if merged:
                 nc.vector.tensor_tensor(slot(k, "h", "hi"), slot(k, "lo", "x1"), slot(k, "mid", "x2"), ALU.max)
+            else:
+                nc.vector.tensor_tensor(slot(k, "hi"), slot(k, "x1"), slot(k, "x2"), ALU.max)
+
+        def lower(k):
             nc.vector.tensor_tensor(slot(k + 1, "lo"), slot(k, "x1"), slot(k, "x2"), ALU.min)
             nc.vector.tensor_tensor(slot(k + 1, "mid"), slot(k, "hi"), slot(k, "x0"), ALU.min)
-            if k not in (0, 3):
-                quantise_h(k - 1)
+
+        def finish(k):
+            nc.vector.tensor_tensor(slot(k + 1, "h"), slot(k + 1, "lo"), slot(k + 1, "mid"), ALU.max)
 
         made = []
 
@@ -225,53 +224,73 @@ def tile_list_median_codeword_repair_kernel(
         def place(i, j0, j1):
             nc.vector.tensor_tensor(pages[i][:].indirect(idx2[:, j0 // 16 : j1 // 16]), y[i][:, j0:j1], wgo_sb[:, j0:j1], ALU.mult)
 
-        out_v = out.rearrange("(c i v) t -> i c v t", i=4, v=4)
-        ready = []
-        for k in range(len(units)):
+        estimates(0)
+        upper(0, False)
+        quantise([x[:] for x in wa_qs[1]], wa16_1[:])
+        lower(0)
+        affine = placed([P, 16], F32, "affine", 10 * KB)
+        wgo_sb = placed([P, S], F32, "wgo_sb", 10 * KB + 64)
+        nc.sync.dma_start(affine[:, 0:4], gd.rearrange("(p i) -> p i", i=4))
+        nc.sync.dma_start(affine[:, 8:12], bd.rearrange("(p i) -> p i", i=4))
+        nc.sync.dma_start(wgo_sb[:], wgo)
+        for k in (1, 2):
+            estimates(k)
+            upper(k, True)
+            lower(k)
+            quantise_h(k - 1)
+        wd16_0 = cast_wd(nc.scalar.copy, wd_raw0, placed([P, 4 * N], BF16, "wd16_0", region_offset(0)))
+        wd16_1 = cast_wd(nc.vector.tensor_copy, wd_raw1, kept([P, 4 * N], BF16, "wd16_1"))
+        finish(2)
+        quantise([x[:] for x in wd_qs[1]], wd16_1[:])
+        quantise_h(2)
+        quantise([x[:] for x in wd_qs[0]], wd16_0[:])
+
+        estimates(3)
+        for i in range(4):
+            back(i, 0, UN)
+        upper(3, False)
+        lower(3)
+        place(0, 0, UN)
+        finish(3)
+        place(1, 0, UN)
+        quantise_h(3)
+        place(2, 0, UN)
+        place(3, 0, UN)
+
+        ready = [(i, UN, WIDE) for i in range(4)]
+        placed_entries = 0
+        for k in range(NARROW_UNITS, last):
             estimates(k)
             pieces = []
-            while ready and sum(j1 - j0 for i, j0, j1 in pieces) < units[k][1] - units[k][0]:
+            while ready and placed_entries < WIDE * (k - NARROW_UNITS + 1):
                 pieces.append(ready.pop(0))
+                placed_entries += pieces[-1][2] - pieces[-1][1]
             for piece in pieces:
                 back(*piece)
-            vote(k)
+            upper(k, k > NARROW_UNITS)
+            lower(k)
+            if k > NARROW_UNITS:
+                quantise_h(k - 1)
             for piece in pieces:
                 place(*piece)
-            if k == 0:
-                quantise([x[:] for x in wa_qs[1]], wa16_1[:])
-                wgo_sb = placed([P, S], F32, "wgo_sb", 66 * KB)
-                nc.sync.dma_start(wgo_sb[:], wgo)
-            if k == 2:
-                wd16_0 = cast_wd(nc.scalar.copy, wd_raw0, kept([P, 4 * N], BF16, "wd16_0"))
-                nc.vector.tensor_tensor(slot(k + 1, "h"), slot(k + 1, "lo"), slot(k + 1, "mid"), ALU.max)
-                wd16_1 = cast_wd(nc.vector.tensor_copy, wd_raw1, placed([P, 4 * N], BF16, "wd16_1", 62 * KB))
-                quantise_h(k)
-                quantise([x[:] for x in wd_qs[0]], wd16_0[:])
-                quantise([x[:] for x in wd_qs[1]], wd16_1[:])
-            if k == 3:
-                g_w.append(placed([P, HALF], U32, "g_hi", 62 * KB))
-                nc.vector.tensor_copy(g_w[1][:], tab[:].indirect(idx[:, HALF // 16 :]))
-            if k == 2 or k > 3 and units[k - 1][2] == 1:
-                j0, j1 = units[max(k - 1, 2)][:2]
-                ready += [(i, j0, j1) for i in range(3 if j1 <= HALF else 2)]
+            if k > NARROW_UNITS and units[k - 1][2] == 1:
+                j0, j1 = units[k - 1][:2]
+                ready += [(i, j0, j1) for i in range(4 if j1 <= HALF else 2)]
 
-        fill = ready + [(3, 0, WIDE)]
-        for piece in fill:
+        estimates(last)
+        for piece in ready:
             back(*piece)
-        place(*fill[0])
-        nc.vector.tensor_tensor(slot(last + 1, "h"), slot(last + 1, "lo"), slot(last + 1, "mid"), ALU.max)
-        place(*fill[1])
+        upper(last, True)
+        lower(last)
+        quantise_h(last - 1)
+        place(*ready[0])
+        finish(last)
+        place(*ready[1])
         quantise_h(last)
-        for piece in fill[2:]:
-            place(*piece)
-        for i in range(2):
-            back(i, S - WIDE, S)
-            place(i, S - WIDE, S)
+        place(*ready[2])
+        out_v = out.rearrange("(p i) t -> i p t", i=4)
+        for i in range(4):
+            j0 = S - WIDE if i < 2 else HALF
+            back(i, j0, S)
+            place(i, j0, S)
             nc.sync.dma_start(out_v[i], pages[i][:])
-        back(2, HALF, S)
-        place(2, HALF, S)
-        nc.sync.dma_start(out_v[2], pages[2][:])
-        back(3, WIDE, HALF)
-        back(3, HALF, S)
-        place(3, WIDE, S)
-        nc.sync.dma_start(out_v[3], pages[3][:])

@@ -45,12 +45,15 @@ def tile_list_median_codeword_repair_kernel(
         idx = kept([P, S // 16], U16, "idx")
         idx2 = kept([P, S // 16], U16, "idx2")
         nc.sync.dma_start(idx[:], offs)
+        nc.sync.dma_start(idx2[:], offs2)
 
         tab_sc = kept([P, T], U8, "tab_sc")
-        w_sc = placed([P, 2 * H], U8, "w_sc", 27 * KB)
-        nc.scalar.dma_start(tab_sc[:].bitcast(I32), tab_scales[0].bitcast(I32).unsqueeze(1).to_broadcast([16, 8, T // 4]))
-        for e, scales in enumerate((wb_scales, wc_scales)):
-            nc.scalar.dma_start(w_sc[:, e * H : (e + 1) * H].bitcast(I32), scales[0].bitcast(I32).unsqueeze(1).to_broadcast([16, 8, H // 4]))
+        w_sc = kept([P, 2 * H], U8, "w_sc")
+        nc.gpsimd.memset(tab_sc[:].bitcast(I32), 0)
+        nc.scalar.dma_start(tab_sc[0:P:8, :].bitcast(I32), tab_scales[0].bitcast(I32))
+        nc.vector.memset(w_sc[:].bitcast(I32), 0)
+        nc.scalar.dma_start(w_sc[0:P:8, 0:H].bitcast(I32), wb_scales[0].bitcast(I32))
+        nc.scalar.dma_start(w_sc[0:P:8, H : 2 * H].bitcast(I32), wc_scales[0].bitcast(I32))
 
         warm = kept([P, 16], F32, "warm")
         nc.gpsimd.memset(warm[:, 0:1], 0.0)
@@ -66,14 +69,13 @@ def tile_list_median_codeword_repair_kernel(
                 nc.sync.dma_start(raw[:, t * N : (t + 1) * N], rows[t])
             return raw
 
-        wa_raw0 = load_wa(0, placed([P, 4 * PASS], F32, "wa_raw0", 2 * KB))
-        wb_raw = placed([P, H // 2], I32, "wb_raw", 0)
-        wc_raw = placed([P, H], I32, "wc_raw", 16 * KB)
+        wa_raw0 = load_wa(0, placed([P, 4 * PASS], F32, "wa_raw0", 20 * KB))
+        tab = placed([P, T], U32, "tab", 8 * KB)
+        wb_raw = kept([P, H // 2], I32, "wb_raw")
+        wc_raw = kept([P, H], I32, "wc_raw")
+        nc.sync.dma_start(tab[:].bitcast(I32), tab_words[0].rearrange("p n t -> p (n t)").bitcast(I32))
         nc.sync.dma_start(wb_raw[:], wb_words[0].bitcast(I32))
         nc.sync.dma_start(wc_raw[:], wc_words[0].rearrange("p n t -> p (n t)").bitcast(I32))
-        tab = kept([P, T], U32, "tab")
-        nc.sync.dma_start(tab[:].bitcast(I32), tab_words[0].rearrange("p n t -> p (n t)").bitcast(I32))
-        nc.sync.dma_start(idx2[:], offs2)
 
         def quantised(name, width):
             return kept([P, width], U32, name + "_q"), kept([P, width], U8, name + "_s")
@@ -100,39 +102,39 @@ def tile_list_median_codeword_repair_kernel(
 
         for i in range(2):
             nc.vector.memset(pages[i][:].bitcast(I32), 0)
+        clear(2, 0)
         g_sc = kept([P, S], U8, "g_sc")
         nc.vector.tensor_copy(g_sc[:], tab_sc[:].indirect(idx[:]))
-        clear(2, 0)
         planes = kept([P, S + 2 * H], U8, "planes")
-        nc.vector.tensor_copy(planes[:, 0:S].bitcast(I32), g_sc[:].bitcast(I32))
-        nc.scalar.copy(
-            planes[:, S:].bitcast(U32).rearrange("p (a t c) -> p a c t", t=4, c=32),
-            w_sc[:].bitcast(U32).rearrange("p (a c t) -> p a c t", t=4, c=32),
+        nc.vector.tensor_copy(
+            planes[:, S:].bitcast(I32).rearrange("p (a t c) -> p a c t", t=4, c=32),
+            w_sc[:].bitcast(I32).rearrange("p (a c t) -> p a c t", t=4, c=32),
         )
+        nc.vector.tensor_copy(planes[:, 0:S].bitcast(I32), g_sc[:].bitcast(I32))
         for r in range(1, 4):
             nc.sync.dma_start(planes[r:P:32, :].bitcast(I32), planes[8 * r : P : 32, :].bitcast(I32))
-        wa16_0 = cast_wa(nc.scalar.copy, wa_raw0, placed([P, 4 * PASS], BF16, "wa16_0", 27 * KB))
-        wb_q = kept([P, H // 2], I32, "wb_q")
-        wc_q = kept([P, H], U32, "wc_q")
-        nc.vector.tensor_copy(
-            wb_q[:].rearrange("p (b t c v) -> p b c t v", b=HB, t=4, v=2),
-            wb_raw[:].rearrange("p (b c t v) -> p b c t v", b=HB, t=4, v=2),
-        )
+        wa16_0 = cast_wa(nc.scalar.copy, wa_raw0, placed([P, 4 * PASS], BF16, "wa16_0", 28 * KB))
         clear(2, 1)
-        clear(3, 0)
+        quantise([x[:] for x in wa_qs[0]], wa16_0[:])
+        wa_raw1 = load_wa(1, placed([P, 4 * PASS], F32, "wa_raw1", 30 * KB))
+        wb_q = kept([P, H // 2], U32, "wb_q")
+        wc_q = kept([P, H], U32, "wc_q")
+        nc.scalar.copy(
+            wb_q[:].rearrange("p (b t c v) -> p b c t v", b=HB, t=4, v=2),
+            wb_raw[:].bitcast(U32).rearrange("p (b c t v) -> p b c t v", b=HB, t=4, v=2),
+        )
         nc.scalar.copy(
             wc_q[:].rearrange("p (b t c v) -> p b c t v", b=HB, t=4, v=4),
             wc_raw[:].bitcast(U32).rearrange("p (b c t v) -> p b c t v", b=HB, t=4, v=4),
         )
-        quantise([x[:] for x in wa_qs[0]], wa16_0[:])
-        wa_raw1 = load_wa(1, placed([P, 4 * PASS], F32, "wa_raw1", 0))
-        wd_raw0 = load_wd(0, placed([P, 4 * N], F32, "wd_raw0", 29 * KB))
-        wd_raw1 = load_wd(1, placed([P, 4 * N], F32, "wd_raw1", 15 * KB))
-        clear(3, 1)
-        g_w = placed([P, S], U32, "g_w", 24 * KB)
+        g_w = kept([P, S], U32, "g_w")
         nc.vector.tensor_copy(g_w[:, 0:WIDE], tab[:].indirect(idx[:, 0 : WIDE // 16]))
         nc.vector.tensor_copy(g_w[:, WIDE:], tab[:].indirect(idx[:, WIDE // 16 :]))
-        wa16_1 = cast_wa(nc.vector.tensor_copy, wa_raw1, placed([P, 4 * PASS], BF16, "wa16_1", 10 * KB))
+        wd_raw0 = load_wd(0, placed([P, 4 * N], F32, "wd_raw0", 4 * KB))
+        wd_raw1 = load_wd(1, placed([P, 4 * N], F32, "wd_raw1", 12 * KB))
+        clear(3, 0)
+        clear(3, 1)
+        wa16_1 = cast_wa(nc.vector.tensor_copy, wa_raw1, placed([P, 4 * PASS], BF16, "wa16_1", 20 * KB))
 
         est_banks = [psum.tile([P, 4, UN], F32, name=f"est_bank{e}") for e in range(6)]
         y_banks = [psum.tile([P, PASS], F32, name=f"y_bank{e}") for e in range(2)]
@@ -164,12 +166,12 @@ def tile_list_median_codeword_repair_kernel(
 
         filled = []
 
-        def estimates(k):
+        def estimates(k, banks=slice(0, 2)):
             j0, j1, b = units[k]
-            for j in range(j0, j1, UN):
+            for j in range(j0, j1, UN)[banks]:
                 rhs = g_w[:, j : j + UN].bitcast(FP8X4)
                 rhs_s = planes[:, j : j + UN]
-                for x in ("x1", "x2", "x0"):
+                for x in ("x0", "x1", "x2") if k == 0 else ("x1", "x2", "x0"):
                     bank = est_banks[len(filled) % len(est_banks)]
                     filled.append(x)
                     for t in range(4):
@@ -228,14 +230,15 @@ def tile_list_median_codeword_repair_kernel(
         upper(0, False)
         quantise([x[:] for x in wa_qs[1]], wa16_1[:])
         lower(0)
-        affine = placed([P, 16], F32, "affine", 10 * KB)
-        wgo_sb = placed([P, S], F32, "wgo_sb", 10 * KB + 64)
+        affine = placed([P, 16], F32, "affine", 20 * KB)
+        wgo_sb = placed([P, S], F32, "wgo_sb", 20 * KB + 64)
         nc.sync.dma_start(affine[:, 0:4], gd.rearrange("(p i) -> p i", i=4))
         nc.sync.dma_start(affine[:, 8:12], bd.rearrange("(p i) -> p i", i=4))
         nc.sync.dma_start(wgo_sb[:], wgo)
         for k in (1, 2):
             estimates(k)
-            upper(k, True)
+            upper(k, False)
+            finish(k - 1)
             lower(k)
             quantise_h(k - 1)
         wd16_0 = cast_wd(nc.scalar.copy, wd_raw0, placed([P, 4 * N], BF16, "wd16_0", region_offset(0)))
@@ -246,6 +249,7 @@ def tile_list_median_codeword_repair_kernel(
         quantise([x[:] for x in wd_qs[0]], wd16_0[:])
 
         estimates(3)
+        estimates(NARROW_UNITS, slice(0, 1))
         for i in range(4):
             back(i, 0, UN)
         upper(3, False)
@@ -260,7 +264,7 @@ def tile_list_median_codeword_repair_kernel(
         ready = [(i, UN, WIDE) for i in range(4)]
         placed_entries = 0
         for k in range(NARROW_UNITS, last):
-            estimates(k)
+            estimates(k, slice(1 if k == NARROW_UNITS else 0, 2))
             pieces = []
             while ready and placed_entries < WIDE * (k - NARROW_UNITS + 1):
                 pieces.append(ready.pop(0))

@@ -23,7 +23,7 @@ UN = 128
 WIDE = 2 * UN
 HALF = S // 2
 NARROW_UNITS = 4
-WIDE_PLACES = 5
+WIDE_PLACES = 4
 KB = 1024
 
 
@@ -69,23 +69,30 @@ def tile_list_median_codeword_repair_kernel(
                 nc.sync.dma_start(raw[:, t * N : (t + 1) * N], rows[t])
             return raw
 
-        wa_raw0 = load_wa(0, placed([P, 4 * PASS], F32, "wa_raw0", 20 * KB))
-        tab = placed([P, T], U32, "tab", 8 * KB)
-        wb_raw = kept([P, H // 2], I32, "wb_raw")
-        wc_raw = kept([P, H], I32, "wc_raw")
-        nc.sync.dma_start(tab[:].bitcast(I32), tab_words[0].rearrange("p n t -> p (n t)").bitcast(I32))
+        wb_raw = placed([P, H // 2], I32, "wb_raw", 3 * KB)
         nc.sync.dma_start(wb_raw[:], wb_words[0].bitcast(I32))
+        tab = placed([P, T], U32, "tab", 16 * KB)
+        nc.sync.dma_start(tab[:].bitcast(I32), tab_words[0].rearrange("p n t -> p (n t)").bitcast(I32))
+        wa_raw0 = load_wa(0, kept([P, 4 * PASS], F32, "wa_raw0"))
+
+        wb_q = kept([P, H // 2], U32, "wb_q")
+        nc.scalar.copy(
+            wb_q[:].rearrange("p (b t c v) -> p b c t v", b=HB, t=4, v=2),
+            wb_raw[:].bitcast(U32).rearrange("p (b c t v) -> p b c t v", b=HB, t=4, v=2),
+        )
+        wc_raw = placed([P, H], I32, "wc_raw", 0)
         nc.sync.dma_start(wc_raw[:], wc_words[0].rearrange("p n t -> p (n t)").bitcast(I32))
+        wa_raw1 = load_wa(1, placed([P, 4 * PASS], F32, "wa_raw1", 4 * KB))
 
         def quantised(name, width):
             return kept([P, width], U32, name + "_q"), kept([P, width], U8, name + "_s")
 
-        def cast_wa(copy, raw, w16):
-            copy(w16[:].rearrange("p (t c v j) -> p t c j v", t=4, v=4, j=4), raw[:].rearrange("p (j c t v) -> p t c j v", j=4, t=4, v=4))
+        def cast_wa(copy, raw, w16, t0=0, t1=4):
+            copy(w16[:].rearrange("p (t c v j) -> p t c j v", t=4, v=4, j=4)[:, t0:t1], raw[:].rearrange("p (j c t v) -> p t c j v", j=4, t=4, v=4)[:, t0:t1])
             return w16
 
-        def cast_wd(copy, raw, w16):
-            copy(w16[:].rearrange("p (i c t) -> p c t i", i=4, t=4), raw[:].rearrange("p (t c i) -> p c t i", t=4, i=4))
+        def cast_wd(copy, raw, w16, c0=0, c1=P):
+            copy(w16[:].rearrange("p (i c t) -> p c t i", i=4, t=4)[:, c0:c1], raw[:].rearrange("p (t c i) -> p c t i", t=4, i=4)[:, c0:c1])
             return w16
 
         def quantise(qs, w16):
@@ -97,44 +104,48 @@ def tile_list_median_codeword_repair_kernel(
 
         pages = [kept([P, T2], F32, f"page{i}") for i in range(4)]
 
-        def clear(i, half):
-            nc.vector.memset(pages[i][:, half * T2 // 2 : (half + 1) * T2 // 2].bitcast(I32), 0)
+        for page in pages:
+            nc.vector.memset(page[:].bitcast(I32), 0)
+        g_w = kept([P, S], U32, "g_w")
 
-        for i in range(2):
-            nc.vector.memset(pages[i][:].bitcast(I32), 0)
-        clear(2, 0)
-        g_sc = kept([P, S], U8, "g_sc")
-        nc.vector.tensor_copy(g_sc[:], tab_sc[:].indirect(idx[:]))
-        planes = kept([P, S + 2 * H], U8, "planes")
-        nc.vector.tensor_copy(
-            planes[:, S:].bitcast(I32).rearrange("p (a t c) -> p a c t", t=4, c=32),
-            w_sc[:].bitcast(I32).rearrange("p (a c t) -> p a c t", t=4, c=32),
-        )
-        nc.vector.tensor_copy(planes[:, 0:S].bitcast(I32), g_sc[:].bitcast(I32))
-        for r in range(1, 4):
-            nc.sync.dma_start(planes[r:P:32, :].bitcast(I32), planes[8 * r : P : 32, :].bitcast(I32))
-        wa16_0 = cast_wa(nc.scalar.copy, wa_raw0, placed([P, 4 * PASS], BF16, "wa16_0", 28 * KB))
-        clear(2, 1)
-        quantise([x[:] for x in wa_qs[0]], wa16_0[:])
-        wa_raw1 = load_wa(1, placed([P, 4 * PASS], F32, "wa_raw1", 30 * KB))
-        wb_q = kept([P, H // 2], U32, "wb_q")
+        def gather_words(j0, j1):
+            nc.vector.tensor_copy(g_w[:, j0:j1], tab[:].indirect(idx[:, j0 // 16 : j1 // 16]))
+
+        gather_words(0, S - WIDE)
+
+        wa16_0 = cast_wa(nc.scalar.copy, wa_raw0, kept([P, 4 * PASS], BF16, "wa16_0"))
         wc_q = kept([P, H], U32, "wc_q")
-        nc.scalar.copy(
-            wb_q[:].rearrange("p (b t c v) -> p b c t v", b=HB, t=4, v=2),
-            wb_raw[:].bitcast(U32).rearrange("p (b c t v) -> p b c t v", b=HB, t=4, v=2),
-        )
         nc.scalar.copy(
             wc_q[:].rearrange("p (b t c v) -> p b c t v", b=HB, t=4, v=4),
             wc_raw[:].bitcast(U32).rearrange("p (b c t v) -> p b c t v", b=HB, t=4, v=4),
         )
-        g_w = kept([P, S], U32, "g_w")
-        nc.vector.tensor_copy(g_w[:, 0:WIDE], tab[:].indirect(idx[:, 0 : WIDE // 16]))
-        nc.vector.tensor_copy(g_w[:, WIDE:], tab[:].indirect(idx[:, WIDE // 16 :]))
-        wd_raw0 = load_wd(0, placed([P, 4 * N], F32, "wd_raw0", 4 * KB))
-        wd_raw1 = load_wd(1, placed([P, 4 * N], F32, "wd_raw1", 12 * KB))
-        clear(3, 0)
-        clear(3, 1)
-        wa16_1 = cast_wa(nc.vector.tensor_copy, wa_raw1, placed([P, 4 * PASS], BF16, "wa16_1", 20 * KB))
+
+        g_sc = kept([P, S], U8, "g_sc")
+        planes = kept([P, 2 * H + S], U8, "planes")
+
+        def gather_scales(j0, j1):
+            nc.vector.tensor_copy(g_sc[:, j0:j1], tab_sc[:].indirect(idx[:, j0 // 16 : j1 // 16]))
+
+        def spread_scales(j0, j1, c0):
+            nc.vector.tensor_copy(planes[:, 2 * H + j0 : 2 * H + j1].bitcast(I32), g_sc[:, j0:j1].bitcast(I32))
+            for r in range(1, 4):
+                nc.sync.dma_start(planes[r:P:32, c0 : 2 * H + j1].bitcast(I32), planes[8 * r : P : 32, c0 : 2 * H + j1].bitcast(I32))
+
+        gather_scales(0, WIDE)
+        nc.vector.tensor_copy(
+            planes[:, 0 : 2 * H].bitcast(I32).rearrange("p (a t c) -> p a c t", t=4, c=32),
+            w_sc[:].bitcast(I32).rearrange("p (a c t) -> p a c t", t=4, c=32),
+        )
+        spread_scales(0, WIDE, 0)
+        gather_words(S - WIDE, S)
+        wd_raw0 = load_wd(0, placed([P, 4 * N], F32, "wd_raw0", 12 * KB))
+        wd_raw1 = load_wd(1, placed([P, 4 * N], F32, "wd_raw1", 20 * KB))
+        gather_scales(WIDE, S)
+        quantise([x[:] for x in wa_qs[0]], wa16_0[:])
+        wa16_1 = cast_wa(nc.scalar.copy, wa_raw1, placed([P, 4 * PASS], BF16, "wa16_1", 32 * KB), 0, 2)
+        cast_wa(nc.vector.tensor_copy, wa_raw1, wa16_1, 2, 4)
+        spread_scales(WIDE, S, 2 * H + WIDE)
+        quantise([x[:] for x in wa_qs[1]], wa16_1[:])
 
         est_banks = [psum.tile([P, 4, UN], F32, name=f"est_bank{e}") for e in range(6)]
         y_banks = [psum.tile([P, PASS], F32, name=f"y_bank{e}") for e in range(2)]
@@ -170,18 +181,18 @@ def tile_list_median_codeword_repair_kernel(
             j0, j1, b = units[k]
             for j in range(j0, j1, UN)[banks]:
                 rhs = g_w[:, j : j + UN].bitcast(FP8X4)
-                rhs_s = planes[:, j : j + UN]
-                for x in ("x0", "x1", "x2") if k == 0 else ("x1", "x2", "x0"):
+                rhs_s = planes[:, 2 * H + j : 2 * H + j + UN]
+                for x in ("x1", "x2", "x0"):
                     bank = est_banks[len(filled) % len(est_banks)]
                     filled.append(x)
                     for t in range(4):
                         c0 = b * PASS + t * P
                         if x == "x1":
                             lhs = wb_q[:, c0 // 2 : (c0 + P) // 2].bitcast(FP4X4)
-                            lhs_s = planes[:, S + c0 : S + c0 + P]
+                            lhs_s = planes[:, c0 : c0 + P]
                         elif x == "x2":
                             lhs = wc_q[:, c0 : c0 + P].bitcast(FP8X4)
-                            lhs_s = planes[:, S + H + c0 : S + H + c0 + P]
+                            lhs_s = planes[:, H + c0 : H + c0 + P]
                         else:
                             lhs = wa_qs[b][0][:, t * P : (t + 1) * P].bitcast(FP8X4)
                             lhs_s = wa_qs[b][1][:, t * P : (t + 1) * P]
@@ -226,27 +237,27 @@ def tile_list_median_codeword_repair_kernel(
         def place(i, j0, j1):
             nc.vector.tensor_tensor(pages[i][:].indirect(idx2[:, j0 // 16 : j1 // 16]), y[i][:, j0:j1], wgo_sb[:, j0:j1], ALU.mult)
 
-        estimates(0)
-        upper(0, False)
-        quantise([x[:] for x in wa_qs[1]], wa16_1[:])
-        lower(0)
-        affine = placed([P, 16], F32, "affine", 20 * KB)
-        wgo_sb = placed([P, S], F32, "wgo_sb", 20 * KB + 64)
+        affine = placed([P, 16], F32, "affine", 32 * KB)
+        wgo_sb = placed([P, S], F32, "wgo_sb", 32 * KB + 64)
         nc.sync.dma_start(affine[:, 0:4], gd.rearrange("(p i) -> p i", i=4))
         nc.sync.dma_start(affine[:, 8:12], bd.rearrange("(p i) -> p i", i=4))
         nc.sync.dma_start(wgo_sb[:], wgo)
+
+        wd16_0 = cast_wd(nc.vector.tensor_copy, wd_raw0, kept([P, 4 * N], BF16, "wd16_0"))
+        estimates(0)
+        upper(0, False)
+        quantise([x[:] for x in wd_qs[0]], wd16_0[:])
+        lower(0)
         for k in (1, 2):
             estimates(k)
             upper(k, False)
             finish(k - 1)
             lower(k)
             quantise_h(k - 1)
-        wd16_0 = cast_wd(nc.scalar.copy, wd_raw0, placed([P, 4 * N], BF16, "wd16_0", region_offset(0)))
         wd16_1 = cast_wd(nc.vector.tensor_copy, wd_raw1, kept([P, 4 * N], BF16, "wd16_1"))
         finish(2)
         quantise([x[:] for x in wd_qs[1]], wd16_1[:])
         quantise_h(2)
-        quantise([x[:] for x in wd_qs[0]], wd16_0[:])
 
         estimates(3)
         estimates(NARROW_UNITS, slice(0, 1))

@@ -55,10 +55,6 @@ def tile_list_median_codeword_repair_kernel(
         nc.scalar.dma_start(w_sc[0:P:8, 0:H].bitcast(I32), wb_scales[0].bitcast(I32))
         nc.scalar.dma_start(w_sc[0:P:8, H : 2 * H].bitcast(I32), wc_scales[0].bitcast(I32))
 
-        warm = kept([P, 16], F32, "warm")
-        nc.gpsimd.memset(warm[:, 0:1], 0.0)
-        nc.scalar.activation(warm[:, 8:9], warm[:, 0:1], IDENT)
-
         def load_wa(b, raw):
             nc.sync.dma_start(raw[:].rearrange("p (j c) -> p j c", j=4), wa.rearrange("(p j) c -> p j c", j=4)[:, :, b * PASS : (b + 1) * PASS])
             return raw

@@ -100,8 +100,9 @@ def tile_list_median_codeword_repair_kernel(
 
         pages = [kept([P, T2], F32, f"page{i}") for i in range(4)]
 
-        for page in pages:
+        for page in pages[:3]:
             nc.vector.memset(page[:].bitcast(I32), 0)
+        nc.vector.memset(pages[3][:, 0 : T2 // 2].bitcast(I32), 0)
         g_w = kept([P, S], U32, "g_w")
 
         def gather_words(j0, j1):
@@ -141,11 +142,12 @@ def tile_list_median_codeword_repair_kernel(
         wa16_1 = cast_wa(nc.scalar.copy, wa_raw1, placed([P, 4 * PASS], BF16, "wa16_1", 32 * KB), 0, 2)
         cast_wa(nc.vector.tensor_copy, wa_raw1, wa16_1, 2, 4)
         spread_scales(WIDE, S, 2 * H + WIDE)
+        nc.vector.memset(pages[3][:, T2 // 2 :].bitcast(I32), 0)
         quantise([x[:] for x in wa_qs[1]], wa16_1[:])
 
         est_banks = [psum.tile([P, 4, UN], F32, name=f"est_bank{e}") for e in range(6)]
         y_banks = [psum.tile([P, PASS], F32, name=f"y_bank{e}") for e in range(2)]
-        units = [(j0, j0 + UN, b) for b in range(HB) for j0 in (0, UN)]
+        units = [(j0, j0 + UN, b) for j0 in (0, UN) for b in range(HB)]
         units += [(j0, j0 + WIDE, b) for j0 in range(WIDE, S, WIDE) for b in range(HB)]
         last = len(units) - 1
         y = [kept([P, S], F32, f"y{i}") for i in range(4)]
@@ -242,25 +244,27 @@ def tile_list_median_codeword_repair_kernel(
         wd16_0 = cast_wd(nc.vector.tensor_copy, wd_raw0, kept([P, 4 * N], BF16, "wd16_0"))
         estimates(0)
         upper(0, False)
-        quantise([x[:] for x in wd_qs[0]], wd16_0[:])
         lower(0)
-        for k in (1, 2):
-            estimates(k)
-            upper(k, False)
-            finish(k - 1)
-            lower(k)
-            quantise_h(k - 1)
+        quantise([x[:] for x in wd_qs[0]], wd16_0[:])
+        estimates(1)
+        upper(1, True)
+        lower(1)
+        quantise_h(0)
         wd16_1 = cast_wd(nc.vector.tensor_copy, wd_raw1, kept([P, 4 * N], BF16, "wd16_1"))
-        finish(2)
+        finish(1)
         quantise([x[:] for x in wd_qs[1]], wd16_1[:])
-        quantise_h(2)
+        quantise_h(1)
 
+        estimates(2)
         estimates(3)
-        estimates(NARROW_UNITS, slice(0, 1))
         for i in range(4):
             back(i, 0, UN)
+        upper(2, False)
+        lower(2)
         upper(3, False)
+        finish(2)
         lower(3)
+        quantise_h(2)
         place(0, 0, UN)
         finish(3)
         place(1, 0, UN)
@@ -268,37 +272,31 @@ def tile_list_median_codeword_repair_kernel(
         place(2, 0, UN)
         place(3, 0, UN)
 
-        ready = [(i, UN, WIDE) for i in range(4)]
-        placed_entries = 0
-        for k in range(NARROW_UNITS, last):
-            estimates(k, slice(1 if k == NARROW_UNITS else 0, 2))
-            pieces = []
-            while ready and placed_entries < WIDE * (k - NARROW_UNITS + 1):
-                pieces.append(ready.pop(0))
-                placed_entries += pieces[-1][2] - pieces[-1][1]
+        second = [(i, UN, WIDE) for i in range(4)]
+        third = [(i, WIDE, HALF) for i in range(4)]
+        fourth = [(i, HALF, HALF + WIDE) for i in range(2)]
+        behind = [second[:2], second[2:], third[:2], third[2:3], [], third[3:] + fourth]
+        apart = (3, 5, last)
+        ahead = (4, 6)
+        for k, pieces in enumerate(behind, NARROW_UNITS):
+            estimates(k, slice(1 if k - 1 in ahead else 0, 2))
+            if k in ahead:
+                estimates(k + 1, slice(0, 1))
             for piece in pieces:
                 back(*piece)
-            upper(k, k > NARROW_UNITS)
+            upper(k, k - 1 not in apart)
             lower(k)
-            if k > NARROW_UNITS:
+            if k - 1 not in apart:
                 quantise_h(k - 1)
+            if k in apart:
+                place(*pieces[0])
+                finish(k)
+                place(*pieces[1])
+                quantise_h(k)
+                pieces = pieces[2:]
             for piece in pieces:
                 place(*piece)
-            if k > NARROW_UNITS and units[k - 1][2] == 1:
-                j0, j1 = units[k - 1][:2]
-                ready += [(i, j0, j1) for i in range(4 if j1 <= HALF else 2)]
 
-        estimates(last)
-        for piece in ready:
-            back(*piece)
-        upper(last, True)
-        lower(last)
-        quantise_h(last - 1)
-        place(*ready[0])
-        finish(last)
-        place(*ready[1])
-        quantise_h(last)
-        place(*ready[2])
         out_v = out.rearrange("(p i) t -> i p t", i=4)
         for i in range(4):
             j0 = S - WIDE if i < 2 else HALF

@@ -73,8 +73,8 @@ def tile_list_median_codeword_repair_kernel(
 
         wb_q = kept([P, H // 2], U32, "wb_q")
         nc.scalar.copy(
-            wb_q[:].rearrange("p (b t c v) -> p b c t v", b=HB, t=4, v=2),
-            wb_raw[:].bitcast(U32).rearrange("p (b c t v) -> p b c t v", b=HB, t=4, v=2),
+            wb_q[:].rearrange("p (b t c v) -> p b t c v", b=HB, t=4, v=2),
+            wb_raw[:].bitcast(U32).rearrange("p (b c t v) -> p b t c v", b=HB, t=4, v=2),
         )
         wc_raw = placed([P, H], I32, "wc_raw", 0)
         nc.sync.dma_start(wc_raw[:], wc_words[0].rearrange("p n t -> p (n t)").bitcast(I32))
@@ -87,8 +87,8 @@ def tile_list_median_codeword_repair_kernel(
             copy(w16[:].rearrange("p (t c v j) -> p t c j v", t=4, v=4, j=4)[:, t0:t1], raw[:].rearrange("p (j c t v) -> p t c j v", j=4, t=4, v=4)[:, t0:t1])
             return w16
 
-        def cast_wd(copy, raw, w16, c0=0, c1=P):
-            copy(w16[:].rearrange("p (i c t) -> p c t i", i=4, t=4)[:, c0:c1], raw[:].rearrange("p (t c i) -> p c t i", t=4, i=4)[:, c0:c1])
+        def cast_wd(copy, raw, w16, i0=0, i1=4):
+            copy(w16[:].rearrange("p (i c v t) -> p i c t v", i=4, v=4, t=4)[:, i0:i1], raw[:].rearrange("p (t c i v) -> p i c t v", t=4, i=4, v=4)[:, i0:i1])
             return w16
 
         def quantise(qs, w16):
@@ -113,8 +113,8 @@ def tile_list_median_codeword_repair_kernel(
         wa16_0 = cast_wa(nc.scalar.copy, wa_raw0, kept([P, 4 * PASS], BF16, "wa16_0"))
         wc_q = kept([P, H], U32, "wc_q")
         nc.scalar.copy(
-            wc_q[:].rearrange("p (b t c v) -> p b c t v", b=HB, t=4, v=4),
-            wc_raw[:].bitcast(U32).rearrange("p (b c t v) -> p b c t v", b=HB, t=4, v=4),
+            wc_q[:].rearrange("p (b t c v) -> p b t c v", b=HB, t=4, v=4),
+            wc_raw[:].bitcast(U32).rearrange("p (b c t v) -> p b t c v", b=HB, t=4, v=4),
         )
 
         g_sc = kept([P, S], U8, "g_sc")
@@ -130,8 +130,8 @@ def tile_list_median_codeword_repair_kernel(
 
         gather_scales(0, WIDE)
         nc.vector.tensor_copy(
-            planes[:, 0 : 2 * H].bitcast(I32).rearrange("p (a t c) -> p a c t", t=4, c=32),
-            w_sc[:].bitcast(I32).rearrange("p (a c t) -> p a c t", t=4, c=32),
+            planes[:, 0 : 2 * H].bitcast(I32).rearrange("p (a t c w) -> p a c t w", t=4, c=8, w=4),
+            w_sc[:].bitcast(I32).rearrange("p (a c w t) -> p a c t w", t=4, c=8, w=4),
         )
         spread_scales(0, WIDE, 0)
         gather_words(S - WIDE, S)
@@ -230,16 +230,19 @@ def tile_list_median_codeword_repair_kernel(
                     start=(b == 0),
                     stop=(b == HB - 1),
                 )
-            nc.scalar.activation(y[i][:, j0:j1], bank[:, 0 : j1 - j0], IDENT, bias=affine[:, 8 + i : 9 + i], scale=affine[:, i : i + 1])
+            nc.scalar.activation(y[i][:, j0:j1], bank[:, 0 : j1 - j0], IDENT, bias=affine[:, 16 * i + 8 : 16 * i + 9], scale=affine[:, 16 * i : 16 * i + 1])
 
         def place(i, j0, j1):
             nc.vector.tensor_tensor(pages[i][:].indirect(idx2[:, j0 // 16 : j1 // 16]), y[i][:, j0:j1], wgo_sb[:, j0:j1], ALU.mult)
 
-        affine = placed([P, 16], F32, "affine", 32 * KB)
-        wgo_sb = placed([P, S], F32, "wgo_sb", 32 * KB + 64)
-        nc.sync.dma_start(affine[:, 0:4], gd.rearrange("(p i) -> p i", i=4))
-        nc.sync.dma_start(affine[:, 8:12], bd.rearrange("(p i) -> p i", i=4))
-        nc.sync.dma_start(wgo_sb[:], wgo)
+        affine = placed([P, 64], F32, "affine", 32 * KB)
+        wgo_sb = placed([P, S], F32, "wgo_sb", 32 * KB + 256)
+        nc.sync.dma_start(wgo_sb[:, 0:WIDE], wgo[:, 0:WIDE])
+        with nc.allow_non_contiguous_dma(reason="one gain and one bias for each partition and page"):
+            for i in range(4):
+                nc.sync.dma_start(affine[:, 16 * i : 16 * i + 1], gd.rearrange("(c i v) -> i c v", i=4, v=4)[i])
+                nc.sync.dma_start(affine[:, 16 * i + 8 : 16 * i + 9], bd.rearrange("(c i v) -> i c v", i=4, v=4)[i])
+        nc.sync.dma_start(wgo_sb[:, WIDE:], wgo[:, WIDE:])
 
         wd16_0 = cast_wd(nc.vector.tensor_copy, wd_raw0, kept([P, 4 * N], BF16, "wd16_0"))
         estimates(0)
@@ -250,7 +253,8 @@ def tile_list_median_codeword_repair_kernel(
         upper(1, True)
         lower(1)
         quantise_h(0)
-        wd16_1 = cast_wd(nc.vector.tensor_copy, wd_raw1, kept([P, 4 * N], BF16, "wd16_1"))
+        wd16_1 = cast_wd(nc.scalar.copy, wd_raw1, kept([P, 4 * N], BF16, "wd16_1"), 0, 2)
+        cast_wd(nc.vector.tensor_copy, wd_raw1, wd16_1, 2, 4)
         finish(1)
         quantise([x[:] for x in wd_qs[1]], wd16_1[:])
         quantise_h(1)
@@ -297,7 +301,7 @@ def tile_list_median_codeword_repair_kernel(
             for piece in pieces:
                 place(*piece)
 
-        out_v = out.rearrange("(p i) t -> i p t", i=4)
+        out_v = out.rearrange("(c i v) t -> i c v t", i=4, v=4)
         for i in range(4):
             j0 = S - WIDE if i < 2 else HALF
             back(i, j0, S)

from contextlib import ExitStack

import concourse.mybir as mybir

K, H, N, T, S, T2 = 512, 1024, 512, 2048, 1024, 2048
FLOPS = 2 * S * (3 * K * H + H * N)

F32 = mybir.dt.float32
BF16 = mybir.dt.bfloat16
I32 = mybir.dt.int32
U32 = mybir.dt.uint32
U16 = mybir.dt.uint16
U8 = mybir.dt.uint8
FP8X4 = mybir.dt.float8_e4m3fn_x4
FP4X4 = mybir.dt.float4_e2m1fn_x4
ALU = mybir.AluOpType
IDENT = mybir.ActivationFunctionType.Identity

P = 128
PASS = 512
HB = H // PASS
UN = 128
WIDE = 2 * UN
HALF = S // 2
NARROW_UNITS = 4
WIDE_PLACES = 4
KB = 1024


def tile_list_median_codeword_repair_kernel(
    tc, tab_words, tab_scales, offs, wa, wb_words, wb_scales, wc_words, wc_scales, wd, gd, bd, wgo, offs2, out
):
    nc = tc.nc
    with ExitStack() as ctx:
        keep = ctx.enter_context(tc.tile_pool(name="keep", bufs=1))
        stage = ctx.enter_context(tc.tile_pool(name="stage", bufs=1))
        psum = ctx.enter_context(tc.psum_pool(name="psum", bufs=1))

        def kept(shape, dtype, name):
            return keep.tile(shape, dtype, name=name, tag=name, align_bytes=64)

        def placed(shape, dtype, name, offset):
            return stage.tile(shape, dtype, name=name, offset=offset, align_bytes=64)

        idx = kept([P, S // 16], U16, "idx")
        idx2 = kept([P, S // 16], U16, "idx2")
        nc.sync.dma_start(idx[:], offs)
        nc.sync.dma_start(idx2[:], offs2)

        tab_sc = kept([P, T], U8, "tab_sc")
        w_sc = kept([P, 2 * H], U8, "w_sc")
        nc.gpsimd.memset(tab_sc[:].bitcast(I32), 0)
        nc.scalar.dma_start(tab_sc[0:P:8, :].bitcast(I32), tab_scales[0].bitcast(I32))
        nc.vector.memset(w_sc[:].bitcast(I32), 0)
        nc.scalar.dma_start(w_sc[0:P:8, 0:H].bitcast(I32), wb_scales[0].bitcast(I32))
        nc.scalar.dma_start(w_sc[0:P:8, H : 2 * H].bitcast(I32), wc_scales[0].bitcast(I32))

        def load_wa(b, raw):
            nc.sync.dma_start(raw[:].rearrange("p (j c) -> p j c", j=4), wa.rearrange("(p j) c -> p j c", j=4)[:, :, b * PASS : (b + 1) * PASS])
            return raw

        def load_wd(b, raw):
            rows = wd[b * PASS : (b + 1) * PASS, :].rearrange("(c t v) n -> t c (v n)", t=4, v=4)
            for t in range(4):
                nc.sync.dma_start(raw[:, t * N : (t + 1) * N], rows[t])
            return raw

        wb_raw = placed([P, H // 2], I32, "wb_raw", 3 * KB)
        nc.sync.dma_start(wb_raw[:], wb_words[0].bitcast(I32))
        tab = placed([P, T], U32, "tab", 16 * KB)
        nc.sync.dma_start(tab[:].bitcast(I32), tab_words[0].rearrange("p n t -> p (n t)").bitcast(I32))
        wa_raw0 = load_wa(0, kept([P, 4 * PASS], F32, "wa_raw0"))

        wb_q = kept([P, H // 2], U32, "wb_q")
        nc.scalar.copy(
            wb_q[:].rearrange("p (b t c v) -> p b t c v", b=HB, t=4, v=2),
            wb_raw[:].bitcast(U32).rearrange("p (b c t v) -> p b t c v", b=HB, t=4, v=2),
        )
        wc_raw = placed([P, H], I32, "wc_raw", 0)
        nc.sync.dma_start(wc_raw[:], wc_words[0].rearrange("p n t -> p (n t)").bitcast(I32))
        wa_raw1 = load_wa(1, placed([P, 4 * PASS], F32, "wa_raw1", 4 * KB))

        def quantised(name, width):
            return kept([P, width], U32, name + "_q"), kept([P, width], U8, name + "_s")

        def cast_wa(copy, raw, w16, t0=0, t1=4):
            copy(w16[:].rearrange("p (t c v j) -> p t c j v", t=4, v=4, j=4)[:, t0:t1], raw[:].rearrange("p (j c t v) -> p t c j v", j=4, t=4, v=4)[:, t0:t1])
            return w16

        def cast_wd(copy, raw, w16, i0=0, i1=4):
            copy(w16[:].rearrange("p (i c v t) -> p i c t v", i=4, v=4, t=4)[:, i0:i1], raw[:].rearrange("p (t c i v) -> p i c t v", t=4, i=4, v=4)[:, i0:i1])
            return w16

        def quantise(qs, w16):
            nc.vector.quantize_mx(qs[0].bitcast(FP8X4), qs[1], w16)

        wa_qs = [quantised(f"wa{b}", PASS) for b in range(HB)]
        wd_qs = [quantised(f"wd{b}", N) for b in range(HB)]
        h_qs = [quantised(f"h{b}", S) for b in range(HB)]

        pages = [kept([P, T2], F32, f"page{i}") for i in range(4)]

        for page in pages[:3]:
            nc.vector.memset(page[:].bitcast(I32), 0)
        nc.vector.memset(pages[3][:, 0 : T2 // 2].bitcast(I32), 0)
        g_w = kept([P, S], U32, "g_w")

        def gather_words(j0, j1):
            nc.vector.tensor_copy(g_w[:, j0:j1], tab[:].indirect(idx[:, j0 // 16 : j1 // 16]))

        gather_words(0, S - WIDE)

        wa16_0 = cast_wa(nc.scalar.copy, wa_raw0, kept([P, 4 * PASS], BF16, "wa16_0"))
        wc_q = kept([P, H], U32, "wc_q")
        nc.scalar.copy(
            wc_q[:].rearrange("p (b t c v) -> p b t c v", b=HB, t=4, v=4),
            wc_raw[:].bitcast(U32).rearrange("p (b c t v) -> p b t c v", b=HB, t=4, v=4),
        )

        g_sc = kept([P, S], U8, "g_sc")
        planes = kept([P, 2 * H + S], U8, "planes")

        def gather_scales(j0, j1):
            nc.vector.tensor_copy(g_sc[:, j0:j1], tab_sc[:].indirect(idx[:, j0 // 16 : j1 // 16]))

        def spread_scales(j0, j1, c0):
            nc.vector.tensor_copy(planes[:, 2 * H + j0 : 2 * H + j1].bitcast(I32), g_sc[:, j0:j1].bitcast(I32))
            for r in range(1, 4):
                nc.sync.dma_start(planes[r:P:32, c0 : 2 * H + j1].bitcast(I32), planes[8 * r : P : 32, c0 : 2 * H + j1].bitcast(I32))

        gather_scales(0, WIDE)
        nc.vector.tensor_copy(
            planes[:, 0 : 2 * H].bitcast(I32).rearrange("p (a t c w) -> p a c t w", t=4, c=8, w=4),
            w_sc[:].bitcast(I32).rearrange("p (a c w t) -> p a c t w", t=4, c=8, w=4),
        )
        spread_scales(0, WIDE, 0)
        gather_words(S - WIDE, S)
        wd_raw0 = load_wd(0, placed([P, 4 * N], F32, "wd_raw0", 12 * KB))
        wd_raw1 = load_wd(1, placed([P, 4 * N], F32, "wd_raw1", 20 * KB))
        gather_scales(WIDE, S)
        quantise([x[:] for x in wa_qs[0]], wa16_0[:])
        wa16_1 = cast_wa(nc.scalar.copy, wa_raw1, placed([P, 4 * PASS], BF16, "wa16_1", 32 * KB), 0, 2)
        cast_wa(nc.vector.tensor_copy, wa_raw1, wa16_1, 2, 4)
        spread_scales(WIDE, S, 2 * H + WIDE)
        nc.vector.memset(pages[3][:, T2 // 2 :].bitcast(I32), 0)
        quantise([x[:] for x in wa_qs[1]], wa16_1[:])

        est_banks = [psum.tile([P, 4, UN], F32, name=f"est_bank{e}") for e in range(6)]
        y_banks = [psum.tile([P, PASS], F32, name=f"y_bank{e}") for e in range(2)]
        units = [(j0, j0 + UN, b) for j0 in (0, UN) for b in range(HB)]
        units += [(j0, j0 + WIDE, b) for j0 in range(WIDE, S, WIDE) for b in range(HB)]
        last = len(units) - 1
        y = [kept([P, S], F32, f"y{i}") for i in range(4)]

        names = ["lo", "x1", "mid", "x2", "h", "hi", "x0"]

        def widths(k):
            before = 4 * (units[k - 1][1] - units[k - 1][0]) if k > 0 else 0
            own = 4 * (units[k][1] - units[k][0]) if k <= last else 0
            return [before, own, before, own, before, own, own]

        def region_offset(k):
            if k < NARROW_UNITS:
                return (38 + max(0, 7 * k - 3)) * KB
            return (63 + 14 * ((k - NARROW_UNITS) % WIDE_PLACES)) * KB

        regions = {}

        def slot(k, first, end=None):
            w = widths(k)
            if k not in regions:
                regions[k] = placed([P, sum(w)], BF16, f"region{k}", region_offset(k))
            a, z = names.index(first), names.index(end or first)
            return regions[k][:, sum(w[:a]) : sum(w[: z + 1])]

        filled = []

        def estimates(k, banks=slice(0, 2)):
            j0, j1, b = units[k]
            for j in range(j0, j1, UN)[banks]:
                rhs = g_w[:, j : j + UN].bitcast(FP8X4)
                rhs_s = planes[:, 2 * H + j : 2 * H + j + UN]
                for x in ("x1", "x2", "x0"):
                    bank = est_banks[len(filled) % len(est_banks)]
                    filled.append(x)
                    for t in range(4):
                        c0 = b * PASS + t * P
                        if x == "x1":
                            lhs = wb_q[:, c0 // 2 : (c0 + P) // 2].bitcast(FP4X4)
                            lhs_s = planes[:, c0 : c0 + P]
                        elif x == "x2":
                            lhs = wc_q[:, c0 : c0 + P].bitcast(FP8X4)
                            lhs_s = planes[:, H + c0 : H + c0 + P]
                        else:
                            lhs = wa_qs[b][0][:, t * P : (t + 1) * P].bitcast(FP8X4)
                            lhs_s = wa_qs[b][1][:, t * P : (t + 1) * P]
                        nc.tensor.matmul_mx(bank[:, t, :], lhsT=lhs, lhsT_scale=lhs_s, rhs=rhs, rhs_scale=rhs_s, start=True, stop=True)
                    into = slot(k, x)[:, 4 * (j - j0) : 4 * (j - j0 + UN)]
                    nc.scalar.copy(into.rearrange("p (n t) -> p n t", t=4), bank[:].rearrange("p t n -> p n t"))

        def quantise_h(k):
            j0, j1, b = units[k]
            quantise([x[:, j0:j1] for x in h_qs[b]], slot(k + 1, "h"))

        def upper(k, merged):
            if merged:
                nc.vector.tensor_tensor(slot(k, "h", "hi"), slot(k, "lo", "x1"), slot(k, "mid", "x2"), ALU.max)
            else:
                nc.vector.tensor_tensor(slot(k, "hi"), slot(k, "x1"), slot(k, "x2"), ALU.max)

        def lower(k):
            nc.vector.tensor_tensor(slot(k + 1, "lo"), slot(k, "x1"), slot(k, "x2"), ALU.min)
            nc.vector.tensor_tensor(slot(k + 1, "mid"), slot(k, "hi"), slot(k, "x0"), ALU.min)

        def finish(k):
            nc.vector.tensor_tensor(slot(k + 1, "h"), slot(k + 1, "lo"), slot(k + 1, "mid"), ALU.max)

        made = []

        def back(i, j0, j1):
            bank = y_banks[len(made) % 2]
            made.append(i)
            for b in range(HB):
                nc.tensor.matmul_mx(
                    bank[:, 0 : j1 - j0],
                    lhsT=wd_qs[b][0][:, i * P : (i + 1) * P].bitcast(FP8X4),
                    lhsT_scale=wd_qs[b][1][:, i * P : (i + 1) * P],
                    rhs=h_qs[b][0][:, j0:j1].bitcast(FP8X4),
                    rhs_scale=h_qs[b][1][:, j0:j1],
                    start=(b == 0),
                    stop=(b == HB - 1),
                )
            nc.scalar.activation(y[i][:, j0:j1], bank[:, 0 : j1 - j0], IDENT, bias=affine[:, 16 * i + 8 : 16 * i + 9], scale=affine[:, 16 * i : 16 * i + 1])

        def place(i, j0, j1):
            nc.vector.tensor_tensor(pages[i][:].indirect(idx2[:, j0 // 16 : j1 // 16]), y[i][:, j0:j1], wgo_sb[:, j0:j1], ALU.mult)

        affine = placed([P, 64], F32, "affine", 32 * KB)
        wgo_sb = placed([P, S], F32, "wgo_sb", 32 * KB + 256)
        nc.sync.dma_start(wgo_sb[:, 0:WIDE], wgo[:, 0:WIDE])
        with nc.allow_non_contiguous_dma(reason="one gain and one bias for each partition and page"):
            for i in range(4):
                nc.sync.dma_start(affine[:, 16 * i : 16 * i + 1], gd.rearrange("(c i v) -> i c v", i=4, v=4)[i])
                nc.sync.dma_start(affine[:, 16 * i + 8 : 16 * i + 9], bd.rearrange("(c i v) -> i c v", i=4, v=4)[i])
        nc.sync.dma_start(wgo_sb[:, WIDE:], wgo[:, WIDE:])

        wd16_0 = cast_wd(nc.vector.tensor_copy, wd_raw0, kept([P, 4 * N], BF16, "wd16_0"))
        estimates(0)
        upper(0, False)
        lower(0)
        quantise([x[:] for x in wd_qs[0]], wd16_0[:])
        estimates(1)
        upper(1, True)
        lower(1)
        quantise_h(0)
        wd16_1 = cast_wd(nc.scalar.copy, wd_raw1, kept([P, 4 * N], BF16, "wd16_1"), 0, 2)
        cast_wd(nc.vector.tensor_copy, wd_raw1, wd16_1, 2, 4)
        finish(1)
        quantise([x[:] for x in wd_qs[1]], wd16_1[:])
        quantise_h(1)

        estimates(2)
        estimates(3)
        for i in range(4):
            back(i, 0, UN)
        upper(2, False)
        lower(2)
        upper(3, False)
        finish(2)
        lower(3)
        quantise_h(2)
        place(0, 0, UN)
        finish(3)
        place(1, 0, UN)
        quantise_h(3)
        place(2, 0, UN)
        place(3, 0, UN)

        second = [(i, UN, WIDE) for i in range(4)]
        third = [(i, WIDE, HALF) for i in range(4)]
        fourth = [(i, HALF, HALF + WIDE) for i in range(2)]
        behind = [second[:2], second[2:], third[:2], third[2:3], [], third[3:] + fourth]
        apart = (3, 5, last)
        ahead = (4, 6)
        for k, pieces in enumerate(behind, NARROW_UNITS):
            estimates(k, slice(1 if k - 1 in ahead else 0, 2))
            if k in ahead:
                estimates(k + 1, slice(0, 1))
            for piece in pieces:
                back(*piece)
            upper(k, k - 1 not in apart)
            lower(k)
            if k - 1 not in apart:
                quantise_h(k - 1)
            if k in apart:
                place(*pieces[0])
                finish(k)
                place(*pieces[1])
                quantise_h(k)
                pieces = pieces[2:]
            for piece in pieces:
                place(*piece)

        out_v = out.rearrange("(c i v) t -> i c v t", i=4, v=4)
        for i in range(4):
            j0 = S - WIDE if i < 2 else HALF
            back(i, j0, S)
            place(i, j0, S)
            nc.sync.dma_start(out_v[i], pages[i][:])
